import numpy as np
import ml_dtypes


def mxq(x, axis, fmt="e4m3"):
    dtype, down = {"e4m3": (ml_dtypes.float8_e4m3fn, 7), "e5m2": (ml_dtypes.float8_e5m2, 14)}[fmt]
    v = np.moveaxis(np.asarray(x, np.float32).astype(ml_dtypes.bfloat16).astype(np.float64), axis, -1)
    blocks = v.reshape(v.shape[:-1] + (-1, 32))
    amax = np.abs(blocks).max(-1, keepdims=True)
    byte = np.maximum(np.where(amax > 0, np.frexp(amax)[1] - 1 + 127, 0) - down, 1)
    scale = np.exp2(byte - 127.0)
    codes = (blocks / scale).astype(np.float32).astype(dtype).astype(np.float64)
    return np.moveaxis((codes * scale).reshape(v.shape), -1, axis)


WIDE = False


def mx_kscale(k):
    if not WIDE:
        return np.ones(k)
    levels = np.array([18, -18])
    if k % 512:
        return np.exp2(np.random.permutation(np.resize(levels, k // 32))).repeat(32)
    a = np.empty((k // 512, 16))
    for p in range(k // 512):
        a[p, :8] = np.random.permutation(np.resize(levels, 8))
        for g in range(8):
            far = levels[np.abs(levels - a[p, g]) >= 10]
            a[p, g + 8] = far[np.random.randint(len(far))]
    return np.exp2(a.ravel()).repeat(32)


def f64(x):
    return np.asarray(x).astype(np.float64)


def striped(idx):
    return np.tile(np.asarray(idx).reshape(-1, 16).T, (8, 1)).astype(np.uint16)


def unstriped(offs):
    return offs[:16].T.reshape(-1).astype(np.int64)


def sig(x):
    return 1.0 / (1.0 + np.exp(-x))


def setup_inputs():
    n = np.random.standard_normal
    uni = np.random.uniform
    idx = np.random.permutation(2048)[:512]
    f_d = mx_kscale(512)
    f_e = mx_kscale(512)
    f_i = np.ones(2048)
    f_i[idx] = mx_kscale(512)
    return {
        "xT": (n((512, 512)) * f_d[:, None]).astype(np.float32),
        "w1": (n((512, 2048)) / np.sqrt(512) / f_d[:, None] * f_i[None, :]).astype(np.float32),
        "dyT": (n((512, 512)) * f_e[:, None]).astype(np.float32),
        "w2": (n((512, 2048)) / np.sqrt(512) / f_e[:, None]).astype(np.float32),
        "us": (uni(0.75, 1.3, (512, 1))).astype(np.float32),
        "ts": np.tile(uni(0.75, 1.3, 2048) / f_i, (128, 1)).astype(np.float32),
        "wt": (uni(0.75, 1.3, (512, 1)) / np.sqrt(512)).astype(np.float32),
        "offs": striped(idx),
    }


def reference(xT, w1, dyT, w2, us, ts, wt, offs):
    idx = unstriped(offs)
    w1_i = f64(w1)[:, idx]
    w2_i = f64(w2)[:, idx]
    ts_i = f64(ts)[:1][:, idx]
    a = mxq(f64(xT), 0, "e4m3").T @ mxq(w1_i, 0, "e4m3")
    z = f64(us) * ts_i * a
    dh = mxq(f64(dyT), 0, "e5m2").T @ mxq(w2_i, 0, "e4m3")
    da = f64(wt) * f64(us) * ts_i * dh * sig(z) * (1.0 + z * (1.0 - sig(z)))
    out = mxq(da, 1, "e5m2") @ mxq(w1_i, 1, "e4m3").T
    return out

@@ -1,0 +1,224 @@
+from contextlib import ExitStack
+
+import concourse.mybir as mybir
+from concourse.masks import make_identity
+
+D, E, R, T, S = 512, 512, 512, 2048, 512
+FLOPS = 3 * 2 * 512 * 512 * 512
+
+F32 = mybir.dt.float32
+BF16 = mybir.dt.bfloat16
+U32 = mybir.dt.uint32
+U16 = mybir.dt.uint16
+U8 = mybir.dt.uint8
+E4M3 = mybir.dt.float8_e4m3fn_x4
+E5M2 = mybir.dt.float8_e5m2_x4
+ACT = mybir.ActivationFunctionType
+ALU = mybir.AluOpType
+
+P = 128
+PACK = 4
+CHUNKS = R // P
+
+
+def tile_attend_gffn_sil_x_kernel(tc, xT, w1, dyT, w2, us, ts, wt, offs, out):
+    nc = tc.nc
+    with ExitStack() as ctx:
+        keep = ctx.enter_context(tc.tile_pool(name="keep", bufs=1))
+        psum = ctx.enter_context(tc.psum_pool(name="psum", bufs=1))
+
+        def sb(name, shape, dtype, tag=None):
+            return keep.tile(shape, dtype, name=name, tag=tag or name, align_bytes=64)
+
+        def bank(tag, name, shape):
+            return psum.tile(shape, F32, name=name, tag=tag)
+
+        offsets = sb("offsets", [P, S // 16], U16)
+        nc.sync.dma_start(offsets[:], offs)
+        w1_rows = w1.rearrange("(p j) t -> p j t", j=PACK)
+        w2_rows = w2.rearrange("(p j) t -> p j t", j=PACK)
+        w1_planes = [sb(f"w1_plane{j}", [P, T], F32) for j in range(PACK)]
+        w2_planes = [sb(f"w2_plane{j}", [P, T], F32) for j in range(PACK)]
+        x_halves = [sb(f"x_half{h}", [P, PACK, R // 2], F32) for h in range(2)]
+        dy_halves = [sb(f"dy_half{h}", [P, PACK, R // 2], F32) for h in range(2)]
+        x_rows = xT.rearrange("(p j) r -> p j r", j=PACK)
+        dy_rows = dyT.rearrange("(p j) r -> p j r", j=PACK)
+
+        row_scales = sb("row_scales", [P, P], F32)
+        nc.gpsimd.memset(row_scales[:], 0.0)
+        ts_cols = sb("ts_cols", [P, T // P], F32)
+        nc.scalar.dma_start(ts_cols[:], ts[0:1, :].rearrange("o (p c) -> (o p) c", p=P))
+        warm = sb("warm", [P, 2], F32)
+        nc.vector.memset(warm[:, 0:1], 0.0)
+        nc.scalar.activation(out=warm[:, 1:2], in_=warm[:, 0:1], func=ACT.Silu)
+
+        nc.sync.dma_start(w1_planes[0][:], w1_rows[:, 0, :])
+        nc.sync.dma_start(row_scales[0:CHUNKS, :], us.rearrange("(c p) o -> c (p o)", p=P))
+        nc.sync.dma_start(row_scales[CHUNKS : 2 * CHUNKS, :], wt.rearrange("(c p) o -> c (p o)", p=P))
+        for j in range(1, PACK):
+            nc.sync.dma_start(w1_planes[j][:], w1_rows[:, j, :])
+        for h in range(2):
+            nc.sync.dma_start(x_halves[h][:], x_rows[:, :, h * (R // 2) : (h + 1) * (R // 2)])
+        for j in range(PACK - 1):
+            nc.sync.dma_start(w2_planes[j][:], w2_rows[:, j, :])
+        for h in range(2):
+            nc.sync.dma_start(dy_halves[h][:], dy_rows[:, :, h * (R // 2) : (h + 1) * (R // 2)])
+        nc.sync.dma_start(w2_planes[PACK - 1][:], w2_rows[:, PACK - 1, :])
+
+        ident = sb("ident", [P, P], F32)
+        make_identity(nc, ident[:])
+
+        ts_window = sb("ts_window", [P, T], F32)
+        ts_view = ts_window[:].rearrange("m (n c) -> m n c", c=T // P)
+        for q in range(4):
+            spread = bank(f"A{q}", f"spread{q}", [P, 4, P])
+            for k in range(4):
+                c = 4 * q + k
+                nc.tensor.transpose(spread[:, k, :], ts_cols[:, c : c + 1].to_broadcast([P, P]), ident[:])
+            nc.scalar.activation(
+                out=ts_view[:, :, 4 * q : 4 * q + 4], in_=spread[:].rearrange("m k n -> m n k"), func=ACT.Copy
+            )
+        turned = bank("B0", "turned", [P, P])
+        nc.tensor.transpose(turned[:], row_scales[:], ident[:])
+        col_scales = sb("col_scales", [P, 2 * CHUNKS], F32)
+        nc.vector.tensor_copy(out=col_scales[:], in_=turned[:, 0 : 2 * CHUNKS])
+        us_cols = col_scales[:, 0:CHUNKS]
+        da_cols = sb("da_cols", [P, CHUNKS], F32)
+        nc.vector.scalar_tensor_tensor(
+            out=da_cols[:], in0=us_cols, scalar=-0.5, in1=col_scales[:, CHUNKS : 2 * CHUNKS], op0=ALU.mult, op1=ALU.mult
+        )
+
+        def gather_plane(pair, planes, j):
+            nc.vector.tensor_copy(out=pair[:, j % 2, :], in_=planes[j][:].indirect(offsets[:]))
+
+        def weave_pair(copy, woven, pair, u):
+            copy(out=woven[:, :, 2 * u : 2 * u + 2], in_=pair[:].rearrange("p j s -> p s j"))
+
+        def quantize(name, woven, width, fmt, tag=None):
+            codes = sb(name + "_codes", [P, width], U32, tag)
+            scales = sb(name + "_scales", [P, width], U8)
+            nc.vector.quantize_mx(out=codes[:].bitcast(fmt), scales=scales[:], in_=woven)
+            return codes[:].bitcast(fmt), scales[:]
+
+        def weave_rows(woven, halves, c):
+            src = halves[c // 2][:, :, (c % 2) * P : (c % 2 + 1) * P]
+            nc.scalar.copy(
+                out=woven.rearrange("p (g i) j -> p g j i", i=4), in_=src.rearrange("p j (g i) -> p g j i", i=4)
+            )
+
+        def rows_half(name, halves, h, fmt):
+            woven = sb(name, [P, 2 * P, PACK], BF16)
+            for k in range(2):
+                weave_rows(woven[:, k * P : (k + 1) * P, :], halves, 2 * h + k)
+            return quantize(name, woven[:].rearrange("p r j -> p (r j)"), 2 * P, fmt)
+
+        w1_pairs = [sb(f"w1_pair{u}", [P, 2, S], BF16) for u in range(2)]
+        w1_woven = sb("w1_woven", [P, S, PACK], BF16)
+        w1_turned = sb("w1_turned", [P, D, PACK], BF16)
+        w1_turned_words = w1_turned[:].rearrange("q d t -> q (d t)").bitcast(F32).rearrange("q (p b k) -> q p b k", b=2, k=4)
+        ts_slots = sb("ts_slots", [P, S], F32)
+        for b in range(2):
+            gather_plane(w1_pairs[b], w1_planes, 2 * b)
+            gather_plane(w1_pairs[b], w1_planes, 2 * b + 1)
+            weave_pair(nc.vector.tensor_copy, w1_woven, w1_pairs[b], b)
+            if b == 0:
+                nc.vector.tensor_copy(out=ts_slots[:], in_=ts_window[:].indirect(offsets[:]))
+            words = w1_pairs[b][:].rearrange("p j s -> p (j s)").bitcast(F32)
+            tb = bank(f"B{1 + b}", f"w1_turn{b}", [P, 4, P])
+            for jj in range(2):
+                for u in range(2):
+                    nc.tensor.transpose(tb[:, 2 * jj + u, :], words[:, 256 * jj + u : 256 * (jj + 1) : 2], ident[:])
+            if b == 1:
+                w1d = quantize("w1d", w1_woven[:].rearrange("p s j -> p (s j)"), S, E4M3)
+            nc.scalar.copy(out=w1_turned_words[:, :, b, :], in_=tb[:].rearrange("q k p -> q p k"))
+
+        ths, ms, tss, fs = [], [], [], []
+        for h in range(2):
+            xq = rows_half(f"x{h}", x_halves, h, E4M3)
+            z = sb(f"z{h}", [P, 2, S], F32)
+            for k in range(2):
+                c = 2 * h + k
+                cols = slice(k * P, (k + 1) * P)
+                a = bank(f"A{c}", f"a{c}", [P, S])
+                nc.tensor.matmul_mx(
+                    out=a[:], lhsT=xq[0][:, cols], lhsT_scale=xq[1][:, cols], rhs=w1d[0], rhs_scale=w1d[1], start=True, stop=True
+                )
+                nc.vector.scalar_tensor_tensor(
+                    out=z[:, k, :], in0=a[:], scalar=us_cols[:, c : c + 1], in1=ts_slots[:], op0=ALU.mult, op1=ALU.mult
+                )
+            th = sb(f"th{h}", [P, 2, S], F32)
+            nc.scalar.activation(out=th[:], in_=z[:], func=ACT.Tanh, scale=0.5)
+            m = sb(f"m{h}", [P, 2, S], F32)
+            nc.scalar.activation(out=m[:], in_=z[:], func=ACT.Silu, scale=-1.0)
+            ths.append(th)
+            ms.append(m)
+
+        w2_pairs = [sb("w2_pair0", [P, 2, S], BF16, "x0_codes"), sb("w2_pair1", [P, 2, S], BF16)]
+        w2_woven = sb("w2_woven", [P, S, PACK], BF16)
+        ts_twice = ts_slots[:].unsqueeze(1).to_broadcast([P, 2, S])
+
+        def first(h, tag):
+            t = sb(f"t{h}", [P, 2, S], F32, tag)
+            nc.vector.scalar_tensor_tensor(out=t[:], in0=ths[h][:], scalar=1.0, in1=ts_twice, op0=ALU.add, op1=ALU.mult)
+            tss.append(t)
+
+        def second(h, tag):
+            f = sb(f"f{h}", [P, 2, S], F32, tag)
+            nc.vector.scalar_tensor_tensor(out=f[:], in0=ms[h][:], scalar=1.0, in1=tss[h][:], op0=ALU.subtract, op1=ALU.mult)
+            fs.extend([f[:, 0, :], f[:, 1, :]])
+
+        gather_plane(w2_pairs[0], w2_planes, 0)
+        first(0, None)
+        w1i = quantize("w1i", w1_turned[:].rearrange("q d t -> q (d t)"), D, E4M3)
+        gather_plane(w2_pairs[0], w2_planes, 1)
+        weave_pair(nc.scalar.copy, w2_woven, w2_pairs[0], 0)
+        second(0, None)
+        gather_plane(w2_pairs[1], w2_planes, 2)
+        dy_woven = sb("dy_woven", [P, R, PACK], BF16)
+        for c in range(CHUNKS):
+            weave_rows(dy_woven[:, c * P : (c + 1) * P, :], dy_halves, c)
+        gather_plane(w2_pairs[1], w2_planes, 3)
+        weave_pair(nc.scalar.copy, w2_woven, w2_pairs[1], 1)
+        dyq = quantize("dy", dy_woven[:].rearrange("p r j -> p (r j)"), R, E5M2, "w2_plane3")
+        first(1, "dy_woven")
+        w2e = quantize("w2e", w2_woven[:].rearrange("p s j -> p (s j)"), S, E4M3)
+        second(1, "w2_woven")
+
+        das = []
+        for h in range(2):
+            for k in range(2):
+                c = 2 * h + k
+                cols = slice(c * P, (c + 1) * P)
+                dh = bank(f"B{c}", f"dh{c}", [P, S])
+                nc.tensor.matmul_mx(
+                    out=dh[:], lhsT=dyq[0][:, cols], lhsT_scale=dyq[1][:, cols], rhs=w2e[0], rhs_scale=w2e[1], start=True, stop=True
+                )
+                das.append(dh)
+
+        def form_da(c):
+            da = sb(f"da{c}", [P, S], BF16)
+            nc.vector.scalar_tensor_tensor(
+                out=da[:], in0=das[c][:], scalar=da_cols[:, c : c + 1], in1=fs[c], op0=ALU.mult, op1=ALU.mult
+            )
+            words = da[:].bitcast(F32)
+            tb = bank(f"B{c}", f"da_turn{c}", [P, 2, P])
+            for u in range(2):
+                nc.tensor.transpose(tb[:, u, :], words[:, u::2], ident[:])
+            woven = sb(f"da_woven{c}", [P, P * PACK], BF16)
+            nc.scalar.copy(out=woven[:].bitcast(F32).rearrange("q (r u) -> q r u", u=2), in_=tb[:].rearrange("q u r -> q r u"))
+            return woven
+
+        def finish(c, woven):
+            daq = quantize(f"daq{c}", woven[:], P, E5M2)
+            acc = bank(f"A{c}", f"acc{c}", [P, D])
+            nc.tensor.matmul_mx(out=acc[:], lhsT=daq[0], lhsT_scale=daq[1], rhs=w1i[0], rhs_scale=w1i[1], start=True, stop=True)
+            res = sb(f"res{c}", [P, D], F32)
+            nc.scalar.copy(out=res[:], in_=acc[:])
+            nc.sync.dma_start(out[c * P : (c + 1) * P, :], res[:])
+
+        wov = []
+        for c in range(CHUNKS):
+            wov.append(form_da(c))
+            if c > 0:
+                finish(c - 1, wov[c - 1])
+        finish(CHUNKS - 1, wov[CHUNKS - 1])

@@ -52,18 +52,16 @@ def tile_attend_gffn_sil_x_kernel(tc, xT, w1, dyT, w2, us, ts, wt, offs, out):
         nc.vector.memset(warm[:, 0:1], 0.0)
         nc.scalar.activation(out=warm[:, 1:2], in_=warm[:, 0:1], func=ACT.Silu)
 
-        nc.sync.dma_start(w1_planes[0][:], w1_rows[:, 0, :])
+        for j in range(PACK):
+            nc.sync.dma_start(w1_planes[j][:], w1_rows[:, j, :])
         nc.sync.dma_start(row_scales[0:CHUNKS, :], us.rearrange("(c p) o -> c (p o)", p=P))
         nc.sync.dma_start(row_scales[CHUNKS : 2 * CHUNKS, :], wt.rearrange("(c p) o -> c (p o)", p=P))
-        for j in range(1, PACK):
-            nc.sync.dma_start(w1_planes[j][:], w1_rows[:, j, :])
         for h in range(2):
             nc.sync.dma_start(x_halves[h][:], x_rows[:, :, h * (R // 2) : (h + 1) * (R // 2)])
-        for j in range(PACK - 1):
+        for j in range(PACK):
             nc.sync.dma_start(w2_planes[j][:], w2_rows[:, j, :])
         for h in range(2):
             nc.sync.dma_start(dy_halves[h][:], dy_rows[:, :, h * (R // 2) : (h + 1) * (R // 2)])
-        nc.sync.dma_start(w2_planes[PACK - 1][:], w2_rows[:, PACK - 1, :])
 
         ident = sb("ident", [P, P], F32)
         make_identity(nc, ident[:])
@@ -83,10 +81,6 @@ def tile_attend_gffn_sil_x_kernel(tc, xT, w1, dyT, w2, us, ts, wt, offs, out):
         col_scales = sb("col_scales", [P, 2 * CHUNKS], F32)
         nc.vector.tensor_copy(out=col_scales[:], in_=turned[:, 0 : 2 * CHUNKS])
         us_cols = col_scales[:, 0:CHUNKS]
-        da_cols = sb("da_cols", [P, CHUNKS], F32)
-        nc.vector.scalar_tensor_tensor(
-            out=da_cols[:], in0=us_cols, scalar=-0.5, in1=col_scales[:, CHUNKS : 2 * CHUNKS], op0=ALU.mult, op1=ALU.mult
-        )
 
         def gather_plane(pair, planes, j):
             nc.vector.tensor_copy(out=pair[:, j % 2, :], in_=planes[j][:].indirect(offsets[:]))
@@ -114,8 +108,18 @@ def tile_attend_gffn_sil_x_kernel(tc, xT, w1, dyT, w2, us, ts, wt, offs, out):
 
         w1_pairs = [sb(f"w1_pair{u}", [P, 2, S], BF16) for u in range(2)]
         w1_woven = sb("w1_woven", [P, S, PACK], BF16)
-        w1_turned = sb("w1_turned", [P, D, PACK], BF16)
-        w1_turned_words = w1_turned[:].rearrange("q d t -> q (d t)").bitcast(F32).rearrange("q (p b k) -> q p b k", b=2, k=4)
+        w1i_codes = sb("w1i_codes", [P, D], U32)
+        w1i_scales = sb("w1i_scales", [P, D], U8)
+        w1i = (w1i_codes[:].bitcast(E4M3), w1i_scales[:])
+
+        def turned_half(b, tb, tag):
+            turned_w1 = sb(f"w1_turned{b}", [P, D // 2 * PACK], BF16, tag)
+            nc.scalar.copy(
+                out=turned_w1[:].bitcast(F32).rearrange("q (p k) -> q p k", k=4), in_=tb[:].rearrange("q k p -> q p k")
+            )
+            cols = slice(b * (D // 2), (b + 1) * (D // 2))
+            nc.vector.quantize_mx(out=w1i[0][:, cols], scales=w1i[1][:, cols], in_=turned_w1[:])
+
         ts_slots = sb("ts_slots", [P, S], F32)
         for b in range(2):
             gather_plane(w1_pairs[b], w1_planes, 2 * b)
@@ -130,12 +134,17 @@ def tile_attend_gffn_sil_x_kernel(tc, xT, w1, dyT, w2, us, ts, wt, offs, out):
                     nc.tensor.transpose(tb[:, 2 * jj + u, :], words[:, 256 * jj + u : 256 * (jj + 1) : 2], ident[:])
             if b == 1:
                 w1d = quantize("w1d", w1_woven[:].rearrange("p s j -> p (s j)"), S, E4M3)
-            nc.scalar.copy(out=w1_turned_words[:, :, b, :], in_=tb[:].rearrange("q k p -> q p k"))
+            if b == 0:
+                turned_half(0, tb, None)
 
         ths, ms, tss, fs = [], [], [], []
+        xqs = [rows_half("x0", x_halves, 0, E4M3)]
+        turned_half(1, tb, "x_half0")
+        xqs.append(rows_half("x1", x_halves, 1, E4M3))
         for h in range(2):
-            xq = rows_half(f"x{h}", x_halves, h, E4M3)
-            z = sb(f"z{h}", [P, 2, S], F32)
+            xq = xqs[h]
+            th = sb(f"th{h}", [P, 2, S], F32)
+            m = sb(f"m{h}", [P, 2, S], F32)
             for k in range(2):
                 c = 2 * h + k
                 cols = slice(k * P, (k + 1) * P)
@@ -143,18 +152,16 @@ def tile_attend_gffn_sil_x_kernel(tc, xT, w1, dyT, w2, us, ts, wt, offs, out):
                 nc.tensor.matmul_mx(
                     out=a[:], lhsT=xq[0][:, cols], lhsT_scale=xq[1][:, cols], rhs=w1d[0], rhs_scale=w1d[1], start=True, stop=True
                 )
+                z = sb(f"z{c}", [P, S], F32, "x1" if c == 1 else None)
                 nc.vector.scalar_tensor_tensor(
-                    out=z[:, k, :], in0=a[:], scalar=us_cols[:, c : c + 1], in1=ts_slots[:], op0=ALU.mult, op1=ALU.mult
+                    out=z[:], in0=a[:], scalar=us_cols[:, c : c + 1], in1=ts_slots[:], op0=ALU.mult, op1=ALU.mult
                 )
-            th = sb(f"th{h}", [P, 2, S], F32)
-            nc.scalar.activation(out=th[:], in_=z[:], func=ACT.Tanh, scale=0.5)
-            m = sb(f"m{h}", [P, 2, S], F32)
-            nc.scalar.activation(out=m[:], in_=z[:], func=ACT.Silu, scale=-1.0)
+                nc.scalar.activation(out=th[:, k, :], in_=z[:], func=ACT.Tanh, scale=0.5)
+                nc.scalar.activation(out=m[:, k, :], in_=z[:], func=ACT.Silu, scale=-1.0)
             ths.append(th)
             ms.append(m)
 
-        w2_pairs = [sb("w2_pair0", [P, 2, S], BF16, "x0_codes"), sb("w2_pair1", [P, 2, S], BF16)]
-        w2_woven = sb("w2_woven", [P, S, PACK], BF16)
+        w2_pairs = [sb("w2_pair0", [P, 2, S], BF16, "x1_codes"), sb("w2_pair1", [P, 2, S], BF16)]
         ts_twice = ts_slots[:].unsqueeze(1).to_broadcast([P, 2, S])
 
         def first(h, tag):
@@ -167,33 +174,50 @@ def tile_attend_gffn_sil_x_kernel(tc, xT, w1, dyT, w2, us, ts, wt, offs, out):
             nc.vector.scalar_tensor_tensor(out=f[:], in0=ms[h][:], scalar=1.0, in1=tss[h][:], op0=ALU.subtract, op1=ALU.mult)
             fs.extend([f[:, 0, :], f[:, 1, :]])
 
+        def weave_half(name, h, tag):
+            woven = sb(name, [P, 2 * P, PACK], BF16, tag)
+            for k in range(2):
+                weave_rows(woven[:, k * P : (k + 1) * P, :], dy_halves, 2 * h + k)
+            return woven[:].rearrange("p r j -> p (r j)")
+
+        w2_woven = sb("w2_woven", [P, S, PACK], BF16)
         gather_plane(w2_pairs[0], w2_planes, 0)
         first(0, None)
-        w1i = quantize("w1i", w1_turned[:].rearrange("q d t -> q (d t)"), D, E4M3)
         gather_plane(w2_pairs[0], w2_planes, 1)
         weave_pair(nc.scalar.copy, w2_woven, w2_pairs[0], 0)
-        second(0, None)
         gather_plane(w2_pairs[1], w2_planes, 2)
-        dy_woven = sb("dy_woven", [P, R, PACK], BF16)
-        for c in range(CHUNKS):
-            weave_rows(dy_woven[:, c * P : (c + 1) * P, :], dy_halves, c)
         gather_plane(w2_pairs[1], w2_planes, 3)
         weave_pair(nc.scalar.copy, w2_woven, w2_pairs[1], 1)
-        dyq = quantize("dy", dy_woven[:].rearrange("p r j -> p (r j)"), R, E5M2, "w2_plane3")
-        first(1, "dy_woven")
+        first(1, "w2_plane3")
+        da_cols = sb("da_cols", [P, CHUNKS], F32, "th1")
+        nc.vector.scalar_tensor_tensor(
+            out=da_cols[:], in0=turned[:, 0:CHUNKS], scalar=-0.5, in1=col_scales[:, CHUNKS : 2 * CHUNKS], op0=ALU.mult, op1=ALU.mult
+        )
+        warm_bank = bank("B0", "warm_bank", [P, S])
+        for rep_i in range(3):
+            nc.tensor.matmul_mx(
+                out=warm_bank[:], lhsT=w1d[0][:, 0:P], lhsT_scale=w1d[1][:, 0:P], rhs=w1d[0], rhs_scale=w1d[1], start=True, stop=True
+            )
+        second(0, "col_scales")
         w2e = quantize("w2e", w2_woven[:].rearrange("p s j -> p (s j)"), S, E4M3)
-        second(1, "w2_woven")
+        dyqs = []
+        for k, tag in enumerate(("w2_woven", None)):
+            f = sb(f"f1{k}", [P, S], F32, tag)
+            nc.vector.scalar_tensor_tensor(
+                out=f[:], in0=ms[1][:, k, :], scalar=1.0, in1=tss[1][:, k, :], op0=ALU.subtract, op1=ALU.mult
+            )
+            fs.append(f[:])
+            dyqs.append(quantize(f"dy{k}", weave_half(f"dy_woven{k}", k, None), 2 * P, E5M2))
 
         das = []
-        for h in range(2):
-            for k in range(2):
-                c = 2 * h + k
-                cols = slice(c * P, (c + 1) * P)
-                dh = bank(f"B{c}", f"dh{c}", [P, S])
-                nc.tensor.matmul_mx(
-                    out=dh[:], lhsT=dyq[0][:, cols], lhsT_scale=dyq[1][:, cols], rhs=w2e[0], rhs_scale=w2e[1], start=True, stop=True
-                )
-                das.append(dh)
+        for c in range(CHUNKS):
+            dyq = dyqs[c // 2]
+            cols = slice((c % 2) * P, (c % 2 + 1) * P)
+            dh = bank(f"B{c}", f"dh{c}", [P, S])
+            nc.tensor.matmul_mx(
+                out=dh[:], lhsT=dyq[0][:, cols], lhsT_scale=dyq[1][:, cols], rhs=w2e[0], rhs_scale=w2e[1], start=True, stop=True
+            )
+            das.append(dh)
 
         def form_da(c):
             da = sb(f"da{c}", [P, S], BF16)
@@ -209,16 +233,24 @@ def tile_attend_gffn_sil_x_kernel(tc, xT, w1, dyT, w2, us, ts, wt, offs, out):
             return woven
 
         def finish(c, woven):
-            daq = quantize(f"daq{c}", woven[:], P, E5M2)
+            daq = quantize(f"daq{c}", woven[:], P, E5M2, ("w2_woven", "f11", None, None)[c])
             acc = bank(f"A{c}", f"acc{c}", [P, D])
             nc.tensor.matmul_mx(out=acc[:], lhsT=daq[0], lhsT_scale=daq[1], rhs=w1i[0], rhs_scale=w1i[1], start=True, stop=True)
-            res = sb(f"res{c}", [P, D], F32)
-            nc.scalar.copy(out=res[:], in_=acc[:])
+            return acc
+
+        def store(c, acc):
+            res = sb(f"res{c}", [P, D], F32, (None, "da3", "da_woven3", None)[c])
+            res_view = res[:].rearrange("r (p b j) -> r p b j", b=2, j=2)
+            acc_view = acc[:].rearrange("r (b p j) -> r p b j", b=2, j=2)
+            if c == 2:
+                nc.vector.tensor_copy(out=res_view, in_=acc_view)
+            else:
+                nc.scalar.copy(out=res_view, in_=acc_view)
             nc.sync.dma_start(out[c * P : (c + 1) * P, :], res[:])
 
-        wov = []
-        for c in range(CHUNKS):
-            wov.append(form_da(c))
-            if c > 0:
-                finish(c - 1, wov[c - 1])
-        finish(CHUNKS - 1, wov[CHUNKS - 1])
+        wov = [form_da(c) for c in range(CHUNKS - 1)]
+        store(0, finish(0, wov[0]))
+        wov.append(form_da(CHUNKS - 1))
+        accs = [finish(c, wov[c]) for c in range(1, CHUNKS)]
+        for c in range(1, CHUNKS):
+            store(c, accs[c - 1])

@@ -139,8 +139,8 @@ def tile_attend_gffn_sil_x_kernel(tc, xT, w1, dyT, w2, us, ts, wt, offs, out):
 
         ths, ms, tss, fs = [], [], [], []
         xqs = [rows_half("x0", x_halves, 0, E4M3)]
-        turned_half(1, tb, "x_half0")
         xqs.append(rows_half("x1", x_halves, 1, E4M3))
+        turned_half(1, tb, "x_half1")
         for h in range(2):
             xq = xqs[h]
             th = sb(f"th{h}", [P, 2, S], F32)
@@ -161,7 +161,7 @@ def tile_attend_gffn_sil_x_kernel(tc, xT, w1, dyT, w2, us, ts, wt, offs, out):
             ths.append(th)
             ms.append(m)
 
-        w2_pairs = [sb("w2_pair0", [P, 2, S], BF16, "x1_codes"), sb("w2_pair1", [P, 2, S], BF16)]
+        w2_pairs = [sb("w2_pair0", [P, 2, S], F32, "x1_codes"), sb("w2_pair1", [P, 2, S], F32)]
         ts_twice = ts_slots[:].unsqueeze(1).to_broadcast([P, 2, S])
 
         def first(h, tag):
@@ -207,7 +207,7 @@ def tile_attend_gffn_sil_x_kernel(tc, xT, w1, dyT, w2, us, ts, wt, offs, out):
                 out=f[:], in0=ms[1][:, k, :], scalar=1.0, in1=tss[1][:, k, :], op0=ALU.subtract, op1=ALU.mult
             )
             fs.append(f[:])
-            dyqs.append(quantize(f"dy{k}", weave_half(f"dy_woven{k}", k, None), 2 * P, E5M2))
+            dyqs.append(quantize(f"dy{k}", weave_half(f"dy_woven{k}", k, (None, "w2_pair1")[k]), 2 * P, E5M2))
 
         das = []
         for c in range(CHUNKS):

@@ -34,7 +34,6 @@ def tile_attend_gffn_sil_x_kernel(tc, xT, w1, dyT, w2, us, ts, wt, offs, out):
             return psum.tile(shape, F32, name=name, tag=tag)
 
         offsets = sb("offsets", [P, S // 16], U16)
-        nc.sync.dma_start(offsets[:], offs)
         w1_rows = w1.rearrange("(p j) t -> p j t", j=PACK)
         w2_rows = w2.rearrange("(p j) t -> p j t", j=PACK)
         w1_planes = [sb(f"w1_plane{j}", [P, T], F32) for j in range(PACK)]
@@ -48,14 +47,16 @@ def tile_attend_gffn_sil_x_kernel(tc, xT, w1, dyT, w2, us, ts, wt, offs, out):
         nc.gpsimd.memset(row_scales[:], 0.0)
         ts_cols = sb("ts_cols", [P, T // P], F32)
         nc.scalar.dma_start(ts_cols[:], ts[0:1, :].rearrange("o (p c) -> (o p) c", p=P))
+        nc.scalar.dma_start(row_scales[0:CHUNKS, :], us.rearrange("(c p) o -> c (p o)", p=P))
+        nc.scalar.dma_start(row_scales[CHUNKS : 2 * CHUNKS, :], wt.rearrange("(c p) o -> c (p o)", p=P))
         warm = sb("warm", [P, 2], F32)
         nc.vector.memset(warm[:, 0:1], 0.0)
         nc.scalar.activation(out=warm[:, 1:2], in_=warm[:, 0:1], func=ACT.Silu)
 
         for j in range(PACK):
             nc.sync.dma_start(w1_planes[j][:], w1_rows[:, j, :])
-        nc.sync.dma_start(row_scales[0:CHUNKS, :], us.rearrange("(c p) o -> c (p o)", p=P))
-        nc.sync.dma_start(row_scales[CHUNKS : 2 * CHUNKS, :], wt.rearrange("(c p) o -> c (p o)", p=P))
+            if j == 0:
+                nc.sync.dma_start(offsets[:], offs)
         for h in range(2):
             nc.sync.dma_start(x_halves[h][:], x_rows[:, :, h * (R // 2) : (h + 1) * (R // 2)])
         for j in range(PACK):
@@ -246,7 +247,8 @@ def tile_attend_gffn_sil_x_kernel(tc, xT, w1, dyT, w2, us, ts, wt, offs, out):
                 nc.vector.tensor_copy(out=res_view, in_=acc_view)
             else:
                 nc.scalar.copy(out=res_view, in_=acc_view)
-            nc.sync.dma_start(out[c * P : (c + 1) * P, :], res[:])
+            queue = nc.scalar if c == CHUNKS - 1 else nc.sync
+            queue.dma_start(out[c * P : (c + 1) * P, :], res[:])
 
         wov = [form_da(c) for c in range(CHUNKS - 1)]
         store(0, finish(0, wov[0]))

@@ -39,7 +39,8 @@ def tile_attend_gffn_sil_x_kernel(tc, xT, w1, dyT, w2, us, ts, wt, offs, out):
         w1_planes = [sb(f"w1_plane{j}", [P, T], F32) for j in range(PACK)]
         w2_planes = [sb(f"w2_plane{j}", [P, T], F32) for j in range(PACK)]
         x_halves = [sb(f"x_half{h}", [P, PACK, R // 2], F32) for h in range(2)]
-        dy_halves = [sb(f"dy_half{h}", [P, PACK, R // 2], F32) for h in range(2)]
+        dy_all = sb("dy_all", [P, PACK, R], F32)
+        dy_halves = [dy_all[:, :, h * (R // 2) : (h + 1) * (R // 2)] for h in range(2)]
         x_rows = xT.rearrange("(p j) r -> p j r", j=PACK)
         dy_rows = dyT.rearrange("(p j) r -> p j r", j=PACK)
 
@@ -50,7 +51,7 @@ def tile_attend_gffn_sil_x_kernel(tc, xT, w1, dyT, w2, us, ts, wt, offs, out):
         nc.scalar.dma_start(row_scales[0:CHUNKS, :], us.rearrange("(c p) o -> c (p o)", p=P))
         nc.scalar.dma_start(row_scales[CHUNKS : 2 * CHUNKS, :], wt.rearrange("(c p) o -> c (p o)", p=P))
         warm = sb("warm", [P, 2], F32)
-        nc.vector.memset(warm[:, 0:1], 0.0)
+        nc.gpsimd.memset(warm[:, 0:1], 0.0)
         nc.scalar.activation(out=warm[:, 1:2], in_=warm[:, 0:1], func=ACT.Silu)
 
         for j in range(PACK):
@@ -61,8 +62,7 @@ def tile_attend_gffn_sil_x_kernel(tc, xT, w1, dyT, w2, us, ts, wt, offs, out):
             nc.sync.dma_start(x_halves[h][:], x_rows[:, :, h * (R // 2) : (h + 1) * (R // 2)])
         for j in range(PACK):
             nc.sync.dma_start(w2_planes[j][:], w2_rows[:, j, :])
-        for h in range(2):
-            nc.sync.dma_start(dy_halves[h][:], dy_rows[:, :, h * (R // 2) : (h + 1) * (R // 2)])
+        nc.sync.dma_start(dy_all[:], dy_rows)
 
         ident = sb("ident", [P, P], F32)
         make_identity(nc, ident[:])
@@ -108,7 +108,7 @@ def tile_attend_gffn_sil_x_kernel(tc, xT, w1, dyT, w2, us, ts, wt, offs, out):
             return quantize(name, woven[:].rearrange("p r j -> p (r j)"), 2 * P, fmt)
 
         w1_pairs = [sb(f"w1_pair{u}", [P, 2, S], BF16) for u in range(2)]
-        w1_woven = sb("w1_woven", [P, S, PACK], BF16)
+        w1_woven = sb("w1_woven", [P, S, PACK], BF16, "ts_cols")
         w1i_codes = sb("w1i_codes", [P, D], U32)
         w1i_scales = sb("w1i_scales", [P, D], U8)
         w1i = (w1i_codes[:].bitcast(E4M3), w1i_scales[:])
@@ -125,7 +125,7 @@ def tile_attend_gffn_sil_x_kernel(tc, xT, w1, dyT, w2, us, ts, wt, offs, out):
         for b in range(2):
             gather_plane(w1_pairs[b], w1_planes, 2 * b)
             gather_plane(w1_pairs[b], w1_planes, 2 * b + 1)
-            weave_pair(nc.vector.tensor_copy, w1_woven, w1_pairs[b], b)
+            weave_pair((nc.scalar.copy, nc.vector.tensor_copy)[b], w1_woven, w1_pairs[b], b)
             if b == 0:
                 nc.vector.tensor_copy(out=ts_slots[:], in_=ts_window[:].indirect(offsets[:]))
             words = w1_pairs[b][:].rearrange("p j s -> p (j s)").bitcast(F32)
@@ -140,12 +140,14 @@ def tile_attend_gffn_sil_x_kernel(tc, xT, w1, dyT, w2, us, ts, wt, offs, out):
 
         ths, ms, tss, fs = [], [], [], []
         xqs = [rows_half("x0", x_halves, 0, E4M3)]
+        turned_half(1, tb, "x_half0")
         xqs.append(rows_half("x1", x_halves, 1, E4M3))
-        turned_half(1, tb, "x_half1")
+        w2_pairs = [sb(f"w2_pair{u}", [P, 2, S], F32) for u in range(2)]
         for h in range(2):
             xq = xqs[h]
             th = sb(f"th{h}", [P, 2, S], F32)
             m = sb(f"m{h}", [P, 2, S], F32)
+            zz = sb(f"z{h}", [P, 2, S], F32, ("x_half1", None)[h])
             for k in range(2):
                 c = 2 * h + k
                 cols = slice(k * P, (k + 1) * P)
@@ -153,26 +155,24 @@ def tile_attend_gffn_sil_x_kernel(tc, xT, w1, dyT, w2, us, ts, wt, offs, out):
                 nc.tensor.matmul_mx(
                     out=a[:], lhsT=xq[0][:, cols], lhsT_scale=xq[1][:, cols], rhs=w1d[0], rhs_scale=w1d[1], start=True, stop=True
                 )
-                z = sb(f"z{c}", [P, S], F32, "x1" if c == 1 else None)
+                z = zz[:, k, :]
                 nc.vector.scalar_tensor_tensor(
-                    out=z[:], in0=a[:], scalar=us_cols[:, c : c + 1], in1=ts_slots[:], op0=ALU.mult, op1=ALU.mult
+                    out=z, in0=a[:], scalar=us_cols[:, c : c + 1], in1=ts_slots[:], op0=ALU.mult, op1=ALU.mult
                 )
-                nc.scalar.activation(out=th[:, k, :], in_=z[:], func=ACT.Tanh, scale=0.5)
-                nc.scalar.activation(out=m[:, k, :], in_=z[:], func=ACT.Silu, scale=-1.0)
+                nc.scalar.activation(out=th[:, k, :], in_=z, func=ACT.Tanh, scale=0.5)
+                nc.scalar.activation(out=m[:, k, :], in_=z, func=ACT.Silu, scale=-1.0)
+            gather_plane(w2_pairs[0], w2_planes, h)
             ths.append(th)
             ms.append(m)
 
-        w2_pairs = [sb("w2_pair0", [P, 2, S], F32, "x1_codes"), sb("w2_pair1", [P, 2, S], F32)]
         ts_twice = ts_slots[:].unsqueeze(1).to_broadcast([P, 2, S])
 
-        def first(h, tag):
-            t = sb(f"t{h}", [P, 2, S], F32, tag)
-            nc.vector.scalar_tensor_tensor(out=t[:], in0=ths[h][:], scalar=1.0, in1=ts_twice, op0=ALU.add, op1=ALU.mult)
+        def first(h, t):
+            nc.vector.scalar_tensor_tensor(out=t, in0=ths[h][:], scalar=1.0, in1=ts_twice, op0=ALU.add, op1=ALU.mult)
             tss.append(t)
 
-        def second(h, tag):
-            f = sb(f"f{h}", [P, 2, S], F32, tag)
-            nc.vector.scalar_tensor_tensor(out=f[:], in0=ms[h][:], scalar=1.0, in1=tss[h][:], op0=ALU.subtract, op1=ALU.mult)
+        def second(h, f):
+            nc.vector.scalar_tensor_tensor(out=f, in0=ms[h][:], scalar=1.0, in1=tss[h], op0=ALU.subtract, op1=ALU.mult)
             fs.extend([f[:, 0, :], f[:, 1, :]])
 
         def weave_half(name, h, tag):
@@ -182,33 +182,37 @@ def tile_attend_gffn_sil_x_kernel(tc, xT, w1, dyT, w2, us, ts, wt, offs, out):
             return woven[:].rearrange("p r j -> p (r j)")
 
         w2_woven = sb("w2_woven", [P, S, PACK], BF16)
-        gather_plane(w2_pairs[0], w2_planes, 0)
-        first(0, None)
-        gather_plane(w2_pairs[0], w2_planes, 1)
         weave_pair(nc.scalar.copy, w2_woven, w2_pairs[0], 0)
+        first(0, sb("t0", [P, 2, S], F32)[:])
         gather_plane(w2_pairs[1], w2_planes, 2)
         gather_plane(w2_pairs[1], w2_planes, 3)
         weave_pair(nc.scalar.copy, w2_woven, w2_pairs[1], 1)
-        first(1, "w2_plane3")
-        da_cols = sb("da_cols", [P, CHUNKS], F32, "th1")
+        late_flat = sb("late", [P, 4 * S + CHUNKS], F32, "w2_plane3")
+        late = late_flat[:, 0 : 4 * S].rearrange("p (k s) -> p k s", k=4)
+        da_cols = late_flat[:, 4 * S : 4 * S + CHUNKS]
+        second(0, late[:, 0:2, :])
         nc.vector.scalar_tensor_tensor(
-            out=da_cols[:], in0=turned[:, 0:CHUNKS], scalar=-0.5, in1=col_scales[:, CHUNKS : 2 * CHUNKS], op0=ALU.mult, op1=ALU.mult
+            out=da_cols, in0=turned[:, 0:CHUNKS], scalar=-0.5, in1=col_scales[:, CHUNKS : 2 * CHUNKS], op0=ALU.mult, op1=ALU.mult
         )
+        first(1, late[:, 2:4, :])
         warm_bank = bank("B0", "warm_bank", [P, S])
         for rep_i in range(3):
             nc.tensor.matmul_mx(
                 out=warm_bank[:], lhsT=w1d[0][:, 0:P], lhsT_scale=w1d[1][:, 0:P], rhs=w1d[0], rhs_scale=w1d[1], start=True, stop=True
             )
-        second(0, "col_scales")
         w2e = quantize("w2e", w2_woven[:].rearrange("p s j -> p (s j)"), S, E4M3)
         dyqs = []
-        for k, tag in enumerate(("w2_woven", None)):
-            f = sb(f"f1{k}", [P, S], F32, tag)
+
+        def second_one(k, f):
             nc.vector.scalar_tensor_tensor(
-                out=f[:], in0=ms[1][:, k, :], scalar=1.0, in1=tss[1][:, k, :], op0=ALU.subtract, op1=ALU.mult
+                out=f, in0=ms[1][:, k, :], scalar=1.0, in1=tss[1][:, k, :], op0=ALU.subtract, op1=ALU.mult
             )
-            fs.append(f[:])
-            dyqs.append(quantize(f"dy{k}", weave_half(f"dy_woven{k}", k, (None, "w2_pair1")[k]), 2 * P, E5M2))
+            fs.append(f)
+
+        dyqs.append(quantize("dy0", weave_half("dy_woven0", 0, None), 2 * P, E5M2))
+        second_one(0, sb("f2", [P, S], F32)[:])
+        second_one(1, sb("f3", [P, S], F32)[:])
+        dyqs.append(quantize("dy1", weave_half("dy_woven1", 1, None), 2 * P, E5M2))
 
         das = []
         for c in range(CHUNKS):
@@ -234,7 +238,7 @@ def tile_attend_gffn_sil_x_kernel(tc, xT, w1, dyT, w2, us, ts, wt, offs, out):
             return woven
 
         def finish(c, woven):
-            daq = quantize(f"daq{c}", woven[:], P, E5M2, ("w2_woven", "f11", None, None)[c])
+            daq = quantize(f"daq{c}", woven[:], P, E5M2, None)
             acc = bank(f"A{c}", f"acc{c}", [P, D])
             nc.tensor.matmul_mx(out=acc[:], lhsT=daq[0], lhsT_scale=daq[1], rhs=w1i[0], rhs_scale=w1i[1], start=True, stop=True)
             return acc

@@ -196,7 +196,7 @@ def tile_attend_gffn_sil_x_kernel(tc, xT, w1, dyT, w2, us, ts, wt, offs, out):
         )
         first(1, late[:, 2:4, :])
         warm_bank = bank("B0", "warm_bank", [P, S])
-        for rep_i in range(3):
+        for rep_i in range(2):
             nc.tensor.matmul_mx(
                 out=warm_bank[:], lhsT=w1d[0][:, 0:P], lhsT_scale=w1d[1][:, 0:P], rhs=w1d[0], rhs_scale=w1d[1], start=True, stop=True
             )
@@ -235,6 +235,11 @@ def tile_attend_gffn_sil_x_kernel(tc, xT, w1, dyT, w2, us, ts, wt, offs, out):
                 nc.tensor.transpose(tb[:, u, :], words[:, u::2], ident[:])
             woven = sb(f"da_woven{c}", [P, P * PACK], BF16)
             nc.scalar.copy(out=woven[:].bitcast(F32).rearrange("q (r u) -> q r u", u=2), in_=tb[:].rearrange("q u r -> q r u"))
+            if c == 0:
+                spare = bank("B0", "spare", [P, S])
+                nc.tensor.matmul_mx(
+                    out=spare[:], lhsT=w1d[0][:, 0:P], lhsT_scale=w1d[1][:, 0:P], rhs=w1d[0], rhs_scale=w1d[1], start=True, stop=True
+                )
             return woven
 
         def finish(c, woven):
@@ -244,19 +249,19 @@ def tile_attend_gffn_sil_x_kernel(tc, xT, w1, dyT, w2, us, ts, wt, offs, out):
             return acc
 
         def store(c, acc):
-            res = sb(f"res{c}", [P, D], F32, (None, "da3", "da_woven3", None)[c])
+            res = sb(f"res{c}", [P, D], F32, (None, "da3", None, None)[c])
             res_view = res[:].rearrange("r (p b j) -> r p b j", b=2, j=2)
             acc_view = acc[:].rearrange("r (b p j) -> r p b j", b=2, j=2)
-            if c == 2:
-                nc.vector.tensor_copy(out=res_view, in_=acc_view)
+            rows = slice(c * P, (c + 1) * P)
+            if c == CHUNKS - 1:
+                for k, queue in enumerate((nc.sync, nc.scalar)):
+                    nc.scalar.copy(out=res_view[:, 64 * k : 64 * (k + 1)], in_=acc_view[:, 64 * k : 64 * (k + 1)])
+                    queue.dma_start(out[rows, 256 * k : 256 * (k + 1)], res[:, 256 * k : 256 * (k + 1)])
             else:
-                nc.scalar.copy(out=res_view, in_=acc_view)
-            queue = nc.scalar if c == CHUNKS - 1 else nc.sync
-            queue.dma_start(out[c * P : (c + 1) * P, :], res[:])
+                (nc.vector.tensor_copy if c % 2 == 0 else nc.scalar.copy)(out=res_view, in_=acc_view)
+                nc.sync.dma_start(out[rows, :], res[:])
 
-        wov = [form_da(c) for c in range(CHUNKS - 1)]
-        store(0, finish(0, wov[0]))
-        wov.append(form_da(CHUNKS - 1))
-        accs = [finish(c, wov[c]) for c in range(1, CHUNKS)]
-        for c in range(1, CHUNKS):
-            store(c, accs[c - 1])
+        wov = [form_da(c) for c in range(CHUNKS)]
+        accs = [finish(c, wov[c]) for c in range(CHUNKS)]
+        for c in range(CHUNKS):
+            store(c, accs[c])

@@ -211,8 +211,8 @@ def tile_attend_gffn_sil_x_kernel(tc, xT, w1, dyT, w2, us, ts, wt, offs, out):
 
         dyqs.append(quantize("dy0", weave_half("dy_woven0", 0, None), 2 * P, E5M2))
         second_one(0, sb("f2", [P, S], F32)[:])
-        second_one(1, sb("f3", [P, S], F32)[:])
         dyqs.append(quantize("dy1", weave_half("dy_woven1", 1, None), 2 * P, E5M2))
+        second_one(1, sb("f3", [P, S], F32, "dy_all")[:])
 
         das = []
         for c in range(CHUNKS):
@@ -225,43 +225,57 @@ def tile_attend_gffn_sil_x_kernel(tc, xT, w1, dyT, w2, us, ts, wt, offs, out):
             das.append(dh)
 
         def form_da(c):
-            da = sb(f"da{c}", [P, S], BF16)
-            nc.vector.scalar_tensor_tensor(
-                out=da[:], in0=das[c][:], scalar=da_cols[:, c : c + 1], in1=fs[c], op0=ALU.mult, op1=ALU.mult
-            )
+            if c == 0:
+                scaled = sb("dh0_scaled", [P, S], F32)
+                nc.scalar.activation(out=scaled[:], in_=das[c][:], func=ACT.Copy, scale=da_cols[:, c : c + 1])
+                da = sb(f"da{c}", [P, S], BF16, "m1")
+                nc.gpsimd.tensor_tensor(out=da[:], in0=scaled[:], in1=fs[c], op=ALU.mult)
+            else:
+                da = sb(f"da{c}", [P, S], BF16)
+                nc.vector.scalar_tensor_tensor(
+                    out=da[:], in0=das[c][:], scalar=da_cols[:, c : c + 1], in1=fs[c], op0=ALU.mult, op1=ALU.mult
+                )
             words = da[:].bitcast(F32)
-            tb = bank(f"B{c}", f"da_turn{c}", [P, 2, P])
+            tb = bank(f"A{c}", f"da_turn{c}", [P, 2, P])
             for u in range(2):
                 nc.tensor.transpose(tb[:, u, :], words[:, u::2], ident[:])
-            woven = sb(f"da_woven{c}", [P, P * PACK], BF16)
-            nc.scalar.copy(out=woven[:].bitcast(F32).rearrange("q (r u) -> q r u", u=2), in_=tb[:].rearrange("q u r -> q r u"))
-            if c == 0:
-                spare = bank("B0", "spare", [P, S])
+            if c == 1:
+                spare = bank("B1", "spare", [P, S])
                 nc.tensor.matmul_mx(
                     out=spare[:], lhsT=w1d[0][:, 0:P], lhsT_scale=w1d[1][:, 0:P], rhs=w1d[0], rhs_scale=w1d[1], start=True, stop=True
                 )
+            woven = sb(f"da_woven{c}", [P, P * PACK], BF16)
+            nc.scalar.copy(out=woven[:].bitcast(F32).rearrange("q (r u) -> q r u", u=2), in_=tb[:].rearrange("q u r -> q r u"))
             return woven
 
         def finish(c, woven):
-            daq = quantize(f"daq{c}", woven[:], P, E5M2, None)
-            acc = bank(f"A{c}", f"acc{c}", [P, D])
+            if c > 0:
+                codes = held_codes[:, (c - 1) * P : c * P].bitcast(E5M2)
+                scales = sb(f"daq{c}_scales", [P, P], U8)
+                nc.vector.quantize_mx(out=codes, scales=scales[:], in_=woven[:])
+                daq = (codes, scales[:])
+            else:
+                daq = quantize(f"daq{c}", woven[:], P, E5M2)
+            acc = bank(f"B{c}", f"acc{c}", [P, D])
             nc.tensor.matmul_mx(out=acc[:], lhsT=daq[0], lhsT_scale=daq[1], rhs=w1i[0], rhs_scale=w1i[1], start=True, stop=True)
             return acc
 
         def store(c, acc):
-            res = sb(f"res{c}", [P, D], F32, (None, "da3", None, None)[c])
+            res = sb(f"res{c}", [P, D], F32, (None, "ident", "da_woven3", None)[c])
             res_view = res[:].rearrange("r (p b j) -> r p b j", b=2, j=2)
             acc_view = acc[:].rearrange("r (b p j) -> r p b j", b=2, j=2)
             rows = slice(c * P, (c + 1) * P)
             if c == CHUNKS - 1:
-                for k, queue in enumerate((nc.sync, nc.scalar)):
-                    nc.scalar.copy(out=res_view[:, 64 * k : 64 * (k + 1)], in_=acc_view[:, 64 * k : 64 * (k + 1)])
+                for k, queue in enumerate((nc.sync, nc.sync)):
+                    nc.vector.tensor_copy(out=res_view[:, 64 * k : 64 * (k + 1)], in_=acc_view[:, 64 * k : 64 * (k + 1)])
                     queue.dma_start(out[rows, 256 * k : 256 * (k + 1)], res[:, 256 * k : 256 * (k + 1)])
             else:
-                (nc.vector.tensor_copy if c % 2 == 0 else nc.scalar.copy)(out=res_view, in_=acc_view)
+                (nc.vector.tensor_copy if c == 2 else nc.scalar.copy)(out=res_view, in_=acc_view)
                 nc.sync.dma_start(out[rows, :], res[:])
 
-        wov = [form_da(c) for c in range(CHUNKS)]
-        accs = [finish(c, wov[c]) for c in range(CHUNKS)]
-        for c in range(CHUNKS):
-            store(c, accs[c])
+        order = (1, 2, 0, 3)
+        wov = [form_da(c) for c in order]
+        held_codes = sb("held_codes", [P, 3 * P], U32, "m1")
+        accs = [finish(c, wov[k]) for k, c in enumerate(order)]
+        for k, c in enumerate(order):
+            store(c, accs[k])

@@ -38,7 +38,8 @@ def tile_attend_gffn_sil_x_kernel(tc, xT, w1, dyT, w2, us, ts, wt, offs, out):
         w2_rows = w2.rearrange("(p j) t -> p j t", j=PACK)
         w1_planes = [sb(f"w1_plane{j}", [P, T], F32) for j in range(PACK)]
         w2_planes = [sb(f"w2_plane{j}", [P, T], F32) for j in range(PACK)]
-        x_halves = [sb(f"x_half{h}", [P, PACK, R // 2], F32) for h in range(2)]
+        x_all = sb("x_all", [P, PACK, R], F32)
+        x_halves = [x_all[:, :, h * (R // 2) : (h + 1) * (R // 2)] for h in range(2)]
         dy_all = sb("dy_all", [P, PACK, R], F32)
         dy_halves = [dy_all[:, :, h * (R // 2) : (h + 1) * (R // 2)] for h in range(2)]
         x_rows = xT.rearrange("(p j) r -> p j r", j=PACK)
@@ -58,8 +59,7 @@ def tile_attend_gffn_sil_x_kernel(tc, xT, w1, dyT, w2, us, ts, wt, offs, out):
             nc.sync.dma_start(w1_planes[j][:], w1_rows[:, j, :])
             if j == 0:
                 nc.sync.dma_start(offsets[:], offs)
-        for h in range(2):
-            nc.sync.dma_start(x_halves[h][:], x_rows[:, :, h * (R // 2) : (h + 1) * (R // 2)])
+        nc.sync.dma_start(x_all[:], x_rows)
         for j in range(PACK):
             nc.sync.dma_start(w2_planes[j][:], w2_rows[:, j, :])
         nc.sync.dma_start(dy_all[:], dy_rows)
@@ -95,16 +95,17 @@ def tile_attend_gffn_sil_x_kernel(tc, xT, w1, dyT, w2, us, ts, wt, offs, out):
             nc.vector.quantize_mx(out=codes[:].bitcast(fmt), scales=scales[:], in_=woven)
             return codes[:].bitcast(fmt), scales[:]
 
-        def weave_rows(woven, halves, c):
+        def weave_rows(woven, halves, c, copy=nc.scalar.copy):
             src = halves[c // 2][:, :, (c % 2) * P : (c % 2 + 1) * P]
-            nc.scalar.copy(
+            copy(
                 out=woven.rearrange("p (g i) j -> p g j i", i=4), in_=src.rearrange("p j (g i) -> p g j i", i=4)
             )
 
         def rows_half(name, halves, h, fmt):
             woven = sb(name, [P, 2 * P, PACK], BF16)
             for k in range(2):
-                weave_rows(woven[:, k * P : (k + 1) * P, :], halves, 2 * h + k)
+                copy = nc.vector.tensor_copy if 2 * h + k == 2 else nc.scalar.copy
+                weave_rows(woven[:, k * P : (k + 1) * P, :], halves, 2 * h + k, copy)
             return quantize(name, woven[:].rearrange("p r j -> p (r j)"), 2 * P, fmt)
 
         w1_pairs = [sb(f"w1_pair{u}", [P, 2, S], BF16) for u in range(2)]
@@ -140,14 +141,14 @@ def tile_attend_gffn_sil_x_kernel(tc, xT, w1, dyT, w2, us, ts, wt, offs, out):
 
         ths, ms, tss, fs = [], [], [], []
         xqs = [rows_half("x0", x_halves, 0, E4M3)]
-        turned_half(1, tb, "x_half0")
         xqs.append(rows_half("x1", x_halves, 1, E4M3))
+        turned_half(1, tb, "x_all")
         w2_pairs = [sb(f"w2_pair{u}", [P, 2, S], F32) for u in range(2)]
         for h in range(2):
             xq = xqs[h]
             th = sb(f"th{h}", [P, 2, S], F32)
             m = sb(f"m{h}", [P, 2, S], F32)
-            zz = sb(f"z{h}", [P, 2, S], F32, ("x_half1", None)[h])
+            zz = sb(f"z{h}", [P, 2, S], F32, None)
             for k in range(2):
                 c = 2 * h + k
                 cols = slice(k * P, (k + 1) * P)

@@ -184,7 +184,12 @@ def tile_attend_gffn_sil_x_kernel(tc, xT, w1, dyT, w2, us, ts, wt, offs, out):
 
         w2_woven = sb("w2_woven", [P, S, PACK], BF16)
         weave_pair(nc.scalar.copy, w2_woven, w2_pairs[0], 0)
-        first(0, sb("t0", [P, 2, S], F32)[:])
+        t0 = sb("t0", [P, 2, S], F32)
+        for k in range(2):
+            th_plus_one = sb(f"th_plus_one{k}", [P, S], F32)
+            nc.gpsimd.tensor_scalar(out=th_plus_one[:], in0=ths[0][:, k, :], scalar1=1.0, scalar2=1.0, op0=ALU.mult, op1=ALU.add)
+            nc.gpsimd.tensor_tensor(out=t0[:, k, :], in0=th_plus_one[:], in1=ts_slots[:], op=ALU.mult)
+        tss.append(t0[:])
         gather_plane(w2_pairs[1], w2_planes, 2)
         gather_plane(w2_pairs[1], w2_planes, 3)
         weave_pair(nc.scalar.copy, w2_woven, w2_pairs[1], 1)

@@ -87,7 +87,10 @@ def tile_attend_gffn_sil_x_kernel(tc, xT, w1, dyT, w2, us, ts, wt, offs, out):
             nc.vector.tensor_copy(out=pair[:, j % 2, :], in_=planes[j][:].indirect(offsets[:]))
 
         def weave_pair(copy, woven, pair, u):
-            copy(out=woven[:, :, 2 * u : 2 * u + 2], in_=pair[:].rearrange("p j s -> p s j"))
+            copy(
+                out=woven[:].rearrange("p (w q e) j -> p q w e j", w=2, e=2)[:, :, :, :, 2 * u : 2 * u + 2],
+                in_=pair[:].rearrange("p j (q w e) -> p q w e j", w=2, e=2),
+            )
 
         def quantize(name, woven, width, fmt, tag=None):
             codes = sb(name + "_codes", [P, width], U32, tag)
@@ -128,7 +131,12 @@ def tile_attend_gffn_sil_x_kernel(tc, xT, w1, dyT, w2, us, ts, wt, offs, out):
             gather_plane(w1_pairs[b], w1_planes, 2 * b + 1)
             weave_pair((nc.scalar.copy, nc.vector.tensor_copy)[b], w1_woven, w1_pairs[b], b)
             if b == 0:
-                nc.vector.tensor_copy(out=ts_slots[:], in_=ts_window[:].indirect(offsets[:]))
+                ts_listed = sb("ts_listed", [P, S], F32)
+                nc.vector.tensor_copy(out=ts_listed[:], in_=ts_window[:].indirect(offsets[:]))
+                nc.vector.tensor_copy(
+                    out=ts_slots[:].rearrange("p (w q e) -> p w q e", w=2, e=2),
+                    in_=ts_listed[:].rearrange("p (q w e) -> p w q e", w=2, e=2),
+                )
             words = w1_pairs[b][:].rearrange("p j s -> p (j s)").bitcast(F32)
             tb = bank(f"B{1 + b}", f"w1_turn{b}", [P, 4, P])
             for jj in range(2):
@@ -244,7 +252,7 @@ def tile_attend_gffn_sil_x_kernel(tc, xT, w1, dyT, w2, us, ts, wt, offs, out):
             words = da[:].bitcast(F32)
             tb = bank(f"A{c}", f"da_turn{c}", [P, 2, P])
             for u in range(2):
-                nc.tensor.transpose(tb[:, u, :], words[:, u::2], ident[:])
+                nc.tensor.transpose(tb[:, u, :], words[:, u * P : (u + 1) * P], ident[:])
             if c == 1:
                 spare = bank("B1", "spare", [P, S])
                 nc.tensor.matmul_mx(

@@ -263,13 +263,7 @@ def tile_attend_gffn_sil_x_kernel(tc, xT, w1, dyT, w2, us, ts, wt, offs, out):
             return woven
 
         def finish(c, woven):
-            if c > 0:
-                codes = held_codes[:, (c - 1) * P : c * P].bitcast(E5M2)
-                scales = sb(f"daq{c}_scales", [P, P], U8)
-                nc.vector.quantize_mx(out=codes, scales=scales[:], in_=woven[:])
-                daq = (codes, scales[:])
-            else:
-                daq = quantize(f"daq{c}", woven[:], P, E5M2)
+            daq = quantize(f"daq{c}", woven[:], P, E5M2)
             acc = bank(f"B{c}", f"acc{c}", [P, D])
             nc.tensor.matmul_mx(out=acc[:], lhsT=daq[0], lhsT_scale=daq[1], rhs=w1i[0], rhs_scale=w1i[1], start=True, stop=True)
             return acc
@@ -279,9 +273,9 @@ def tile_attend_gffn_sil_x_kernel(tc, xT, w1, dyT, w2, us, ts, wt, offs, out):
             res_view = res[:].rearrange("r (p b j) -> r p b j", b=2, j=2)
             acc_view = acc[:].rearrange("r (b p j) -> r p b j", b=2, j=2)
             rows = slice(c * P, (c + 1) * P)
-            if c == CHUNKS - 1:
+            if c in (1, CHUNKS - 1):
                 for k, queue in enumerate((nc.sync, nc.sync)):
-                    nc.vector.tensor_copy(out=res_view[:, 64 * k : 64 * (k + 1)], in_=acc_view[:, 64 * k : 64 * (k + 1)])
+                    (nc.scalar.copy if c == 1 else nc.vector.tensor_copy)(out=res_view[:, 64 * k : 64 * (k + 1)], in_=acc_view[:, 64 * k : 64 * (k + 1)])
                     queue.dma_start(out[rows, 256 * k : 256 * (k + 1)], res[:, 256 * k : 256 * (k + 1)])
             else:
                 (nc.vector.tensor_copy if c == 2 else nc.scalar.copy)(out=res_view, in_=acc_view)
@@ -289,7 +283,6 @@ def tile_attend_gffn_sil_x_kernel(tc, xT, w1, dyT, w2, us, ts, wt, offs, out):
 
         order = (1, 2, 0, 3)
         wov = [form_da(c) for c in order]
-        held_codes = sb("held_codes", [P, 3 * P], U32, "m1")
         accs = [finish(c, wov[k]) for k, c in enumerate(order)]
         for k, c in enumerate(order):
             store(c, accs[k])

@@ -225,13 +225,19 @@ def tile_attend_gffn_sil_x_kernel(tc, xT, w1, dyT, w2, us, ts, wt, offs, out):
 
         dyqs.append(quantize("dy0", weave_half("dy_woven0", 0, None), 2 * P, E5M2))
         second_one(0, sb("f2", [P, S], F32)[:])
-        dyqs.append(quantize("dy1", weave_half("dy_woven1", 1, None), 2 * P, E5M2))
+        late_woven = []
+        for c in (2, 3):
+            woven = sb(f"dy_woven{c}", [P, P, PACK], BF16)
+            weave_rows(woven[:], dy_halves, c)
+            late_woven.append(woven[:].rearrange("p r j -> p (r j)"))
+        dyqs.append(quantize("dy2", late_woven[0], P, E5M2))
         second_one(1, sb("f3", [P, S], F32, "dy_all")[:])
+        dyqs.append(quantize("dy3", late_woven[1], P, E5M2))
 
         das = []
         for c in range(CHUNKS):
-            dyq = dyqs[c // 2]
-            cols = slice((c % 2) * P, (c % 2 + 1) * P)
+            dyq = dyqs[max(c - 1, 0)]
+            cols = slice(P, 2 * P) if c == 1 else slice(0, P)
             dh = bank(f"B{c}", f"dh{c}", [P, S])
             nc.tensor.matmul_mx(
                 out=dh[:], lhsT=dyq[0][:, cols], lhsT_scale=dyq[1][:, cols], rhs=w2e[0], rhs_scale=w2e[1], start=True, stop=True
@@ -242,7 +248,7 @@ def tile_attend_gffn_sil_x_kernel(tc, xT, w1, dyT, w2, us, ts, wt, offs, out):
             if c == 0:
                 scaled = sb("dh0_scaled", [P, S], F32)
                 nc.scalar.activation(out=scaled[:], in_=das[c][:], func=ACT.Copy, scale=da_cols[:, c : c + 1])
-                da = sb(f"da{c}", [P, S], BF16, "m1")
+                da = sb(f"da{c}", [P, S], BF16, "dy_woven3")
                 nc.gpsimd.tensor_tensor(out=da[:], in0=scaled[:], in1=fs[c], op=ALU.mult)
             else:
                 da = sb(f"da{c}", [P, S], BF16)
@@ -250,7 +256,7 @@ def tile_attend_gffn_sil_x_kernel(tc, xT, w1, dyT, w2, us, ts, wt, offs, out):
                     out=da[:], in0=das[c][:], scalar=da_cols[:, c : c + 1], in1=fs[c], op0=ALU.mult, op1=ALU.mult
                 )
             words = da[:].bitcast(F32)
-            tb = bank(f"A{c}", f"da_turn{c}", [P, 2, P])
+            tb = bank(f"A{max(c, 1)}", f"da_turn{c}", [P, 2, P])
             for u in range(2):
                 nc.tensor.transpose(tb[:, u, :], words[:, u * P : (u + 1) * P], ident[:])
             if c == 1:

@@ -79,9 +79,10 @@ def tile_attend_gffn_sil_x_kernel(tc, xT, w1, dyT, w2, us, ts, wt, offs, out):
             )
         turned = bank("B0", "turned", [P, P])
         nc.tensor.transpose(turned[:], row_scales[:], ident[:])
-        col_scales = sb("col_scales", [P, 2 * CHUNKS], F32)
-        nc.vector.tensor_copy(out=col_scales[:], in_=turned[:, 0 : 2 * CHUNKS])
-        us_cols = col_scales[:, 0:CHUNKS]
+        us_cols = sb("us_cols", [P, CHUNKS], F32)
+        wt_cols = sb("wt_cols", [P, CHUNKS], F32)
+        nc.vector.tensor_copy(out=us_cols[:], in_=turned[:, 0:CHUNKS])
+        nc.vector.tensor_copy(out=wt_cols[:], in_=turned[:, CHUNKS : 2 * CHUNKS])
 
         def gather_plane(pair, planes, j):
             nc.vector.tensor_copy(out=pair[:, j % 2, :], in_=planes[j][:].indirect(offsets[:]))
@@ -104,26 +105,16 @@ def tile_attend_gffn_sil_x_kernel(tc, xT, w1, dyT, w2, us, ts, wt, offs, out):
                 out=woven.rearrange("p (g i) j -> p g j i", i=4), in_=src.rearrange("p j (g i) -> p g j i", i=4)
             )
 
-        def rows_half(name, halves, h, fmt):
-            woven = sb(name, [P, 2 * P, PACK], BF16)
-            for k in range(2):
-                copy = nc.vector.tensor_copy if 2 * h + k == 2 else nc.scalar.copy
-                weave_rows(woven[:, k * P : (k + 1) * P, :], halves, 2 * h + k, copy)
-            return quantize(name, woven[:].rearrange("p r j -> p (r j)"), 2 * P, fmt)
-
         w1_pairs = [sb(f"w1_pair{u}", [P, 2, S], BF16) for u in range(2)]
         w1_woven = sb("w1_woven", [P, S, PACK], BF16, "ts_cols")
-        w1i_codes = sb("w1i_codes", [P, D], U32)
-        w1i_scales = sb("w1i_scales", [P, D], U8)
-        w1i = (w1i_codes[:].bitcast(E4M3), w1i_scales[:])
+        w1i = []
 
         def turned_half(b, tb, tag):
             turned_w1 = sb(f"w1_turned{b}", [P, D // 2 * PACK], BF16, tag)
             nc.scalar.copy(
                 out=turned_w1[:].bitcast(F32).rearrange("q (p k) -> q p k", k=4), in_=tb[:].rearrange("q k p -> q p k")
             )
-            cols = slice(b * (D // 2), (b + 1) * (D // 2))
-            nc.vector.quantize_mx(out=w1i[0][:, cols], scales=w1i[1][:, cols], in_=turned_w1[:])
+            return turned_w1
 
         ts_slots = sb("ts_slots", [P, S], F32)
         for b in range(2):
@@ -145,34 +136,43 @@ def tile_attend_gffn_sil_x_kernel(tc, xT, w1, dyT, w2, us, ts, wt, offs, out):
             if b == 1:
                 w1d = quantize("w1d", w1_woven[:].rearrange("p s j -> p (s j)"), S, E4M3)
             if b == 0:
-                turned_half(0, tb, None)
+                w1i.append(quantize("w1i0", turned_half(0, tb, None)[:], D // 2, E4M3))
 
         ths, ms, tss, fs = [], [], [], []
-        xqs = [rows_half("x0", x_halves, 0, E4M3)]
-        xqs.append(rows_half("x1", x_halves, 1, E4M3))
-        turned_half(1, tb, "x_all")
-        w2_pairs = [sb(f"w2_pair{u}", [P, 2, S], F32) for u in range(2)]
-        for h in range(2):
-            xq = xqs[h]
-            th = sb(f"th{h}", [P, 2, S], F32)
-            m = sb(f"m{h}", [P, 2, S], F32)
-            zz = sb(f"z{h}", [P, 2, S], F32, None)
-            for k in range(2):
-                c = 2 * h + k
-                cols = slice(k * P, (k + 1) * P)
-                a = bank(f"A{c}", f"a{c}", [P, S])
-                nc.tensor.matmul_mx(
-                    out=a[:], lhsT=xq[0][:, cols], lhsT_scale=xq[1][:, cols], rhs=w1d[0], rhs_scale=w1d[1], start=True, stop=True
-                )
-                z = zz[:, k, :]
-                nc.vector.scalar_tensor_tensor(
-                    out=z, in0=a[:], scalar=us_cols[:, c : c + 1], in1=ts_slots[:], op0=ALU.mult, op1=ALU.mult
-                )
-                nc.scalar.activation(out=th[:, k, :], in_=z, func=ACT.Tanh, scale=0.5)
-                nc.scalar.activation(out=m[:, k, :], in_=z, func=ACT.Silu, scale=-1.0)
-            gather_plane(w2_pairs[0], w2_planes, h)
-            ths.append(th)
-            ms.append(m)
+        x_first = sb("x_first", [P, P, PACK], BF16, "w1_plane3")
+        x_middle = sb("x_middle", [P, 2 * P, PACK], BF16, "w1_plane2")
+        x_woven = [x_first[:], x_middle[:, 0:P, :], x_middle[:, P : 2 * P, :]]
+        for c in range(3):
+            weave_rows(x_woven[c], x_halves, c)
+        zzs = [sb(f"z{h}", [P, 2, S], F32) for h in range(2)]
+        ths.extend([sb(f"th{h}", [P, 2, S], F32) for h in range(2)])
+        ms.extend([sb(f"m{h}", [P, 2, S], F32) for h in range(2)])
+
+        def first_product(c):
+            xq = quantize(f"xq{c}", x_woven[c].rearrange("p r j -> p (r j)"), P, E4M3)
+            a = bank(f"A{c}", f"a{c}", [P, S])
+            nc.tensor.matmul_mx(out=a[:], lhsT=xq[0], lhsT_scale=xq[1], rhs=w1d[0], rhs_scale=w1d[1], start=True, stop=True)
+            return a
+
+        def form_z(c, a):
+            h, k = divmod(c, 2)
+            z = zzs[h][:, k, :]
+            nc.vector.scalar_tensor_tensor(out=z, in0=a[:], scalar=us_cols[:, c : c + 1], in1=ts_slots[:], op0=ALU.mult, op1=ALU.mult)
+            nc.scalar.activation(out=ths[h][:, k, :], in_=z, func=ACT.Tanh, scale=0.5)
+            nc.scalar.activation(out=ms[h][:, k, :], in_=z, func=ACT.Silu, scale=-1.0)
+
+        a0 = first_product(0)
+        x_last = sb("x_last", [P, P, PACK], BF16, "w1_plane3")
+        x_woven.append(x_last[:])
+        weave_rows(x_woven[3], x_halves, 3, nc.vector.tensor_copy)
+        turned1 = turned_half(1, tb, "xq0_codes")
+        a1 = first_product(1)
+        form_z(0, a0)
+        a3 = first_product(3)
+        a2 = first_product(2)
+        form_z(1, a1)
+        form_z(2, a2)
+        form_z(3, a3)
 
         ts_twice = ts_slots[:].unsqueeze(1).to_broadcast([P, 2, S])
 
@@ -184,60 +184,56 @@ def tile_attend_gffn_sil_x_kernel(tc, xT, w1, dyT, w2, us, ts, wt, offs, out):
             nc.vector.scalar_tensor_tensor(out=f, in0=ms[h][:], scalar=1.0, in1=tss[h], op0=ALU.subtract, op1=ALU.mult)
             fs.extend([f[:, 0, :], f[:, 1, :]])
 
-        def weave_half(name, h, tag):
-            woven = sb(name, [P, 2 * P, PACK], BF16, tag)
-            for k in range(2):
-                weave_rows(woven[:, k * P : (k + 1) * P, :], dy_halves, 2 * h + k)
-            return woven[:].rearrange("p r j -> p (r j)")
-
-        w2_woven = sb("w2_woven", [P, S, PACK], BF16)
-        weave_pair(nc.scalar.copy, w2_woven, w2_pairs[0], 0)
+        w2_listed = sb("w2_listed", [P, PACK, S], BF16, "us_cols")
+        for j in range(2):
+            nc.vector.tensor_copy(out=w2_listed[:, j, :], in_=w2_planes[j][:].indirect(offsets[:]))
+        for j in range(2, PACK):
+            nc.scalar.activation(out=w2_listed[:, j, :], in_=w2_planes[j][:].indirect(offsets[:]), func=ACT.Copy)
         t0 = sb("t0", [P, 2, S], F32)
         for k in range(2):
             th_plus_one = sb(f"th_plus_one{k}", [P, S], F32)
             nc.gpsimd.tensor_scalar(out=th_plus_one[:], in0=ths[0][:, k, :], scalar1=1.0, scalar2=1.0, op0=ALU.mult, op1=ALU.add)
             nc.gpsimd.tensor_tensor(out=t0[:, k, :], in0=th_plus_one[:], in1=ts_slots[:], op=ALU.mult)
         tss.append(t0[:])
-        gather_plane(w2_pairs[1], w2_planes, 2)
-        gather_plane(w2_pairs[1], w2_planes, 3)
-        weave_pair(nc.scalar.copy, w2_woven, w2_pairs[1], 1)
-        late_flat = sb("late", [P, 4 * S + CHUNKS], F32, "w2_plane3")
-        late = late_flat[:, 0 : 4 * S].rearrange("p (k s) -> p k s", k=4)
-        da_cols = late_flat[:, 4 * S : 4 * S + CHUNKS]
-        second(0, late[:, 0:2, :])
-        nc.vector.scalar_tensor_tensor(
-            out=da_cols, in0=turned[:, 0:CHUNKS], scalar=-0.5, in1=col_scales[:, CHUNKS : 2 * CHUNKS], op0=ALU.mult, op1=ALU.mult
-        )
-        first(1, late[:, 2:4, :])
+        first(1, sb("t1", [P, 2, S], F32)[:])
+        second(0, sb("f0", [P, 2, S], F32)[:])
+        w2_woven = sb("w2_woven", [P, S, PACK], BF16)
+        for copy, part in ((nc.vector.tensor_copy, slice(0, 96)), (nc.scalar.copy, slice(96, P))):
+            copy(
+                out=w2_woven[:].rearrange("p (w q e) j -> p q w e j", w=2, e=2)[:, part],
+                in_=w2_listed[:].rearrange("p j (q w e) -> p q w e j", w=2, e=2)[:, part],
+            )
+        late = sb("late", [P, 2 * S + CHUNKS], F32, "w2_plane3")
+        da_cols = late[:, 2 * S : 2 * S + CHUNKS]
+        nc.vector.scalar_tensor_tensor(out=da_cols, in0=turned[:, 0:CHUNKS], scalar=-0.5, in1=wt_cols[:], op0=ALU.mult, op1=ALU.mult)
         warm_bank = bank("B0", "warm_bank", [P, S])
         for rep_i in range(2):
             nc.tensor.matmul_mx(
                 out=warm_bank[:], lhsT=w1d[0][:, 0:P], lhsT_scale=w1d[1][:, 0:P], rhs=w1d[0], rhs_scale=w1d[1], start=True, stop=True
             )
-        w2e = quantize("w2e", w2_woven[:].rearrange("p s j -> p (s j)"), S, E4M3)
-        dyqs = []
+        dy_woven = sb("dy_woven", [P, R, PACK], BF16, "z1")
+        for c in range(CHUNKS):
+            weave_rows(dy_woven[:, c * P : (c + 1) * P, :], dy_halves, c)
 
-        def second_one(k, f):
-            nc.vector.scalar_tensor_tensor(
-                out=f, in0=ms[1][:, k, :], scalar=1.0, in1=tss[1][:, k, :], op0=ALU.subtract, op1=ALU.mult
-            )
+        def quantize_dy(h, tag=None):
+            return quantize(f"dy{h}", dy_woven[:, 2 * h * P : 2 * (h + 1) * P, :].rearrange("p r j -> p (r j)"), 2 * P, E5M2, tag)
+
+        def second_one(k):
+            f = late[:, k * S : (k + 1) * S]
+            nc.vector.scalar_tensor_tensor(out=f, in0=ms[1][:, k, :], scalar=1.0, in1=tss[1][:, k, :], op0=ALU.subtract, op1=ALU.mult)
             fs.append(f)
 
-        dyqs.append(quantize("dy0", weave_half("dy_woven0", 0, None), 2 * P, E5M2))
-        second_one(0, sb("f2", [P, S], F32)[:])
-        late_woven = []
-        for c in (2, 3):
-            woven = sb(f"dy_woven{c}", [P, P, PACK], BF16)
-            weave_rows(woven[:], dy_halves, c)
-            late_woven.append(woven[:].rearrange("p r j -> p (r j)"))
-        dyqs.append(quantize("dy2", late_woven[0], P, E5M2))
-        second_one(1, sb("f3", [P, S], F32, "dy_all")[:])
-        dyqs.append(quantize("dy3", late_woven[1], P, E5M2))
+        second_one(0)
+        w2e = quantize("w2e", w2_woven[:].rearrange("p s j -> p (s j)"), S, E4M3)
+        second_one(1)
+        dyqs = [quantize_dy(0)]
+        w1i.append(quantize("w1i1", turned1[:], D // 2, E4M3, "us_cols"))
+        dyqs.append(quantize_dy(1))
 
         das = []
         for c in range(CHUNKS):
-            dyq = dyqs[max(c - 1, 0)]
-            cols = slice(P, 2 * P) if c == 1 else slice(0, P)
+            dyq = dyqs[c // 2]
+            cols = slice((c % 2) * P, (c % 2 + 1) * P)
             dh = bank(f"B{c}", f"dh{c}", [P, S])
             nc.tensor.matmul_mx(
                 out=dh[:], lhsT=dyq[0][:, cols], lhsT_scale=dyq[1][:, cols], rhs=w2e[0], rhs_scale=w2e[1], start=True, stop=True
@@ -248,7 +244,7 @@ def tile_attend_gffn_sil_x_kernel(tc, xT, w1, dyT, w2, us, ts, wt, offs, out):
             if c == 0:
                 scaled = sb("dh0_scaled", [P, S], F32)
                 nc.scalar.activation(out=scaled[:], in_=das[c][:], func=ACT.Copy, scale=da_cols[:, c : c + 1])
-                da = sb(f"da{c}", [P, S], BF16, "dy_woven3")
+                da = sb(f"da{c}", [P, S], BF16, "z1")
                 nc.gpsimd.tensor_tensor(out=da[:], in0=scaled[:], in1=fs[c], op=ALU.mult)
             else:
                 da = sb(f"da{c}", [P, S], BF16)
@@ -271,7 +267,10 @@ def tile_attend_gffn_sil_x_kernel(tc, xT, w1, dyT, w2, us, ts, wt, offs, out):
         def finish(c, woven):
             daq = quantize(f"daq{c}", woven[:], P, E5M2)
             acc = bank(f"B{c}", f"acc{c}", [P, D])
-            nc.tensor.matmul_mx(out=acc[:], lhsT=daq[0], lhsT_scale=daq[1], rhs=w1i[0], rhs_scale=w1i[1], start=True, stop=True)
+            for b in range(2):
+                nc.tensor.matmul_mx(
+                    out=acc[:, b * 2 * P : (b + 1) * 2 * P], lhsT=daq[0], lhsT_scale=daq[1], rhs=w1i[b][0], rhs_scale=w1i[b][1], start=True, stop=True
+                )
             return acc
 
         def store(c, acc):

@@ -206,11 +206,6 @@ def tile_attend_gffn_sil_x_kernel(tc, xT, w1, dyT, w2, us, ts, wt, offs, out):
         late = sb("late", [P, 2 * S + CHUNKS], F32, "w2_plane3")
         da_cols = late[:, 2 * S : 2 * S + CHUNKS]
         nc.vector.scalar_tensor_tensor(out=da_cols, in0=turned[:, 0:CHUNKS], scalar=-0.5, in1=wt_cols[:], op0=ALU.mult, op1=ALU.mult)
-        warm_bank = bank("B0", "warm_bank", [P, S])
-        for rep_i in range(2):
-            nc.tensor.matmul_mx(
-                out=warm_bank[:], lhsT=w1d[0][:, 0:P], lhsT_scale=w1d[1][:, 0:P], rhs=w1d[0], rhs_scale=w1d[1], start=True, stop=True
-            )
         dy_woven = sb("dy_woven", [P, R, PACK], BF16, "z1")
         for c in range(CHUNKS):
             weave_rows(dy_woven[:, c * P : (c + 1) * P, :], dy_halves, c)
@@ -255,11 +250,6 @@ def tile_attend_gffn_sil_x_kernel(tc, xT, w1, dyT, w2, us, ts, wt, offs, out):
             tb = bank(f"A{max(c, 1)}", f"da_turn{c}", [P, 2, P])
             for u in range(2):
                 nc.tensor.transpose(tb[:, u, :], words[:, u * P : (u + 1) * P], ident[:])
-            if c == 1:
-                spare = bank("B1", "spare", [P, S])
-                nc.tensor.matmul_mx(
-                    out=spare[:], lhsT=w1d[0][:, 0:P], lhsT_scale=w1d[1][:, 0:P], rhs=w1d[0], rhs_scale=w1d[1], start=True, stop=True
-                )
             woven = sb(f"da_woven{c}", [P, P * PACK], BF16)
             nc.scalar.copy(out=woven[:].bitcast(F32).rearrange("q (r u) -> q r u", u=2), in_=tb[:].rearrange("q u r -> q r u"))
             return woven

@@ -30,68 +30,43 @@ def tile_attend_gffn_sil_x_kernel(tc, xT, w1, dyT, w2, us, ts, wt, offs, out):
         def sb(name, shape, dtype, tag=None):
             return keep.tile(shape, dtype, name=name, tag=tag or name, align_bytes=64)
 
-        def bank(tag, name, shape):
-            return psum.tile(shape, F32, name=name, tag=tag)
+        placed = ctx.enter_context(tc.tile_pool(name="placed", bufs=1))
+
+        def at(offset, name, shape, dtype):
+            return placed.tile(shape, dtype, name=name, align_bytes=64, offset=offset)
+
+        def bank(number, name, shape):
+            return psum.tile(shape, F32, name=name, tag=f"bank{number}")
 
         offsets = sb("offsets", [P, S // 16], U16)
         w1_rows = w1.rearrange("(p j) t -> p j t", j=PACK)
         w2_rows = w2.rearrange("(p j) t -> p j t", j=PACK)
         w1_planes = [sb(f"w1_plane{j}", [P, T], F32) for j in range(PACK)]
         w2_planes = [sb(f"w2_plane{j}", [P, T], F32) for j in range(PACK)]
-        x_all = sb("x_all", [P, PACK, R], F32)
-        x_halves = [x_all[:, :, h * (R // 2) : (h + 1) * (R // 2)] for h in range(2)]
-        dy_all = sb("dy_all", [P, PACK, R], F32)
-        dy_halves = [dy_all[:, :, h * (R // 2) : (h + 1) * (R // 2)] for h in range(2)]
-        x_rows = xT.rearrange("(p j) r -> p j r", j=PACK)
-        dy_rows = dyT.rearrange("(p j) r -> p j r", j=PACK)
+        x_raw = sb("x_raw", [P, PACK, R], F32)
+        dy_raw = sb("dy_raw", [P, PACK, R], F32)
+        us_cols = sb("us_cols", [P, PACK], F32)
+        wt_cols = sb("wt_cols", [P, PACK], F32)
+        ts_window = sb("ts_window", [P, T], F32)
 
-        row_scales = sb("row_scales", [P, P], F32)
-        nc.gpsimd.memset(row_scales[:], 0.0)
-        ts_cols = sb("ts_cols", [P, T // P], F32)
-        nc.scalar.dma_start(ts_cols[:], ts[0:1, :].rearrange("o (p c) -> (o p) c", p=P))
-        nc.scalar.dma_start(row_scales[0:CHUNKS, :], us.rearrange("(c p) o -> c (p o)", p=P))
-        nc.scalar.dma_start(row_scales[CHUNKS : 2 * CHUNKS, :], wt.rearrange("(c p) o -> c (p o)", p=P))
+        ts_pieces = sb("ts_pieces", [P, T // P], F32)
+        nc.scalar.dma_start(ts_pieces[:], ts[0:1, :].rearrange("o (p c) -> (o p) c", p=P))
+        nc.scalar.dma_start(us_cols[:], us.rearrange("(p c) o -> p (c o)", c=PACK))
+        nc.scalar.dma_start(wt_cols[:], wt.rearrange("(p c) o -> p (c o)", c=PACK))
         warm = sb("warm", [P, 2], F32)
         nc.gpsimd.memset(warm[:, 0:1], 0.0)
         nc.scalar.activation(out=warm[:, 1:2], in_=warm[:, 0:1], func=ACT.Silu)
 
+        nc.sync.dma_start(x_raw[:], xT.rearrange("(p j) r -> p j r", j=PACK))
+        nc.sync.dma_start(offsets[:], offs)
         for j in range(PACK):
             nc.sync.dma_start(w1_planes[j][:], w1_rows[:, j, :])
-            if j == 0:
-                nc.sync.dma_start(offsets[:], offs)
-        nc.sync.dma_start(x_all[:], x_rows)
+        nc.sync.dma_start(dy_raw[:], dyT.rearrange("(p j) r -> p j r", j=PACK))
         for j in range(PACK):
             nc.sync.dma_start(w2_planes[j][:], w2_rows[:, j, :])
-        nc.sync.dma_start(dy_all[:], dy_rows)
 
         ident = sb("ident", [P, P], F32)
         make_identity(nc, ident[:])
-
-        ts_window = sb("ts_window", [P, T], F32)
-        ts_view = ts_window[:].rearrange("m (n c) -> m n c", c=T // P)
-        for q in range(4):
-            spread = bank(f"A{q}", f"spread{q}", [P, 4, P])
-            for k in range(4):
-                c = 4 * q + k
-                nc.tensor.transpose(spread[:, k, :], ts_cols[:, c : c + 1].to_broadcast([P, P]), ident[:])
-            nc.scalar.activation(
-                out=ts_view[:, :, 4 * q : 4 * q + 4], in_=spread[:].rearrange("m k n -> m n k"), func=ACT.Copy
-            )
-        turned = bank("B0", "turned", [P, P])
-        nc.tensor.transpose(turned[:], row_scales[:], ident[:])
-        us_cols = sb("us_cols", [P, CHUNKS], F32)
-        wt_cols = sb("wt_cols", [P, CHUNKS], F32)
-        nc.vector.tensor_copy(out=us_cols[:], in_=turned[:, 0:CHUNKS])
-        nc.vector.tensor_copy(out=wt_cols[:], in_=turned[:, CHUNKS : 2 * CHUNKS])
-
-        def gather_plane(pair, planes, j):
-            nc.vector.tensor_copy(out=pair[:, j % 2, :], in_=planes[j][:].indirect(offsets[:]))
-
-        def weave_pair(copy, woven, pair, u):
-            copy(
-                out=woven[:].rearrange("p (w q e) j -> p q w e j", w=2, e=2)[:, :, :, :, 2 * u : 2 * u + 2],
-                in_=pair[:].rearrange("p j (q w e) -> p q w e j", w=2, e=2),
-            )
 
         def quantize(name, woven, width, fmt, tag=None):
             codes = sb(name + "_codes", [P, width], U32, tag)
@@ -99,185 +74,168 @@ def tile_attend_gffn_sil_x_kernel(tc, xT, w1, dyT, w2, us, ts, wt, offs, out):
             nc.vector.quantize_mx(out=codes[:].bitcast(fmt), scales=scales[:], in_=woven)
             return codes[:].bitcast(fmt), scales[:]
 
-        def weave_rows(woven, halves, c, copy=nc.scalar.copy):
-            src = halves[c // 2][:, :, (c % 2) * P : (c % 2 + 1) * P]
+        def product(acc, stationary, s_cols, moving, m_cols):
+            nc.tensor.matmul_mx(
+                out=acc, lhsT=stationary[0][:, s_cols], lhsT_scale=stationary[1][:, s_cols],
+                rhs=moving[0][:, m_cols], rhs_scale=moving[1][:, m_cols], start=True, stop=True,
+            )
+
+        def cols(k, width=P):
+            return slice(k * width, (k + 1) * width)
+
+        ts_view = ts_window[:].rearrange("m (n c) -> m n c", c=T // P)
+        for g in range(4):
+            spread = bank(g, f"spread{g}", [P, 4, P])
+            for k in range(4):
+                c = 4 * g + k
+                nc.tensor.transpose(spread[:, k, :], ts_pieces[:, c : c + 1].to_broadcast([P, P]), ident[:])
+            nc.scalar.activation(out=ts_view[:, :, 4 * g : 4 * g + 4], in_=spread[:].rearrange("m k n -> m n k"), func=ACT.Copy)
+
+        c_cols = sb("c_cols", [P, PACK], F32)
+        half_us = sb("half_us", [P, PACK], F32)
+        nc.gpsimd.tensor_scalar(out=half_us[:], in0=us_cols[:], scalar1=-0.5, scalar2=0.0, op0=ALU.mult, op1=ALU.add)
+        nc.gpsimd.tensor_tensor(out=c_cols[:], in0=half_us[:], in1=wt_cols[:], op=ALU.mult)
+        us_spread = bank(4, "us_spread", [P, PACK, P])
+        c_spread = bank(5, "c_spread", [P, PACK, P])
+        for spread, source in ((us_spread, us_cols), (c_spread, c_cols)):
+            for c in range(PACK):
+                nc.tensor.transpose(spread[:, c, :], source[:, c : c + 1].to_broadcast([P, P]), ident[:])
+        us_row = sb("us_row", [P, R], F32)
+        nc.scalar.copy(out=us_row[:].rearrange("m (p c) -> m p c", c=PACK), in_=us_spread[:].rearrange("m c p -> m p c"))
+        c_row = sb("c_row", [P, R], F32)
+        nc.scalar.copy(out=c_row[:].rearrange("m (p c) -> m p c", c=PACK), in_=c_spread[:].rearrange("m c p -> m p c"))
+
+        x_woven = sb("x_woven", [P, R, PACK], BF16)
+        nc.vector.tensor_copy(
+            out=x_woven[:].rearrange("p (g i) j -> p g j i", i=4), in_=x_raw[:].rearrange("p j (g i) -> p g j i", i=4)
+        )
+        ts_listed = at(2048, "ts_listed", [P, S], F32)
+        nc.scalar.activation(out=ts_listed[:], in_=ts_window[:].indirect(offsets[:]), func=ACT.Copy)
+        xq = quantize("xq", x_woven[:].rearrange("p r j -> p (r j)"), R, E4M3)
+        ts_turn = bank(6, "ts_turn", [P, PACK, P])
+        for t in range(PACK):
+            nc.tensor.transpose(ts_turn[:, t, :], ts_listed[:, t : S : PACK], ident[:])
+        ts_cols = sb("ts_cols", [P, PACK], F32)
+        nc.scalar.copy(out=ts_cols[:], in_=ts_turn[:, :, 0])
+        table = sb("table", [P, PACK, R], F32)
+        for t in range(PACK):
+            nc.gpsimd.tensor_scalar(out=table[:, t, :], in0=c_row[:], scalar1=ts_cols[:, t : t + 1], scalar2=0.0, op0=ALU.mult, op1=ALU.add)
+
+        w1_pairs = [at(64 * u, f"w1_pair{u}", [P, 2, S], BF16) for u in range(2)]
+        w1_woven = sb("w1_woven", [P, S, PACK], BF16)
+
+        def weave(copy, woven, listed, places, planes, part=slice(0, P)):
             copy(
-                out=woven.rearrange("p (g i) j -> p g j i", i=4), in_=src.rearrange("p j (g i) -> p g j i", i=4)
+                out=woven[:].rearrange("p (t q) j -> p q t j", t=PACK)[:, part, places, planes],
+                in_=listed[:].rearrange("p j (q t) -> p q t j", t=PACK)[:, part, places, :],
             )
 
-        w1_pairs = [sb(f"w1_pair{u}", [P, 2, S], BF16) for u in range(2)]
-        w1_woven = sb("w1_woven", [P, S, PACK], BF16, "ts_cols")
-        w1i = []
-
-        def turned_half(b, tb, tag):
-            turned_w1 = sb(f"w1_turned{b}", [P, D // 2 * PACK], BF16, tag)
-            nc.scalar.copy(
-                out=turned_w1[:].bitcast(F32).rearrange("q (p k) -> q p k", k=4), in_=tb[:].rearrange("q k p -> q p k")
-            )
-            return turned_w1
-
-        ts_slots = sb("ts_slots", [P, S], F32)
-        for b in range(2):
-            gather_plane(w1_pairs[b], w1_planes, 2 * b)
-            gather_plane(w1_pairs[b], w1_planes, 2 * b + 1)
-            weave_pair((nc.scalar.copy, nc.vector.tensor_copy)[b], w1_woven, w1_pairs[b], b)
-            if b == 0:
-                ts_listed = sb("ts_listed", [P, S], F32)
-                nc.vector.tensor_copy(out=ts_listed[:], in_=ts_window[:].indirect(offsets[:]))
-                nc.vector.tensor_copy(
-                    out=ts_slots[:].rearrange("p (w q e) -> p w q e", w=2, e=2),
-                    in_=ts_listed[:].rearrange("p (q w e) -> p w q e", w=2, e=2),
-                )
+        def turn(b, number):
             words = w1_pairs[b][:].rearrange("p j s -> p (j s)").bitcast(F32)
-            tb = bank(f"B{1 + b}", f"w1_turn{b}", [P, 4, P])
+            tb = bank(number, f"w1_turn{b}", [P, 4, P])
             for jj in range(2):
                 for u in range(2):
                     nc.tensor.transpose(tb[:, 2 * jj + u, :], words[:, 256 * jj + u : 256 * (jj + 1) : 2], ident[:])
-            if b == 1:
-                w1d = quantize("w1d", w1_woven[:].rearrange("p s j -> p (s j)"), S, E4M3)
-            if b == 0:
-                w1i.append(quantize("w1i0", turned_half(0, tb, None)[:], D // 2, E4M3))
+            turned = sb(f"w1_turned{b}", [P, D // 2 * PACK], BF16)
+            nc.scalar.copy(out=turned[:].bitcast(F32).rearrange("q (p k) -> q p k", k=4), in_=tb[:].rearrange("q k p -> q p k"))
+            return turned
 
-        ths, ms, tss, fs = [], [], [], []
-        x_first = sb("x_first", [P, P, PACK], BF16, "w1_plane3")
-        x_middle = sb("x_middle", [P, 2 * P, PACK], BF16, "w1_plane2")
-        x_woven = [x_first[:], x_middle[:, 0:P, :], x_middle[:, P : 2 * P, :]]
-        for c in range(3):
-            weave_rows(x_woven[c], x_halves, c)
-        zzs = [sb(f"z{h}", [P, 2, S], F32) for h in range(2)]
-        ths.extend([sb(f"th{h}", [P, 2, S], F32) for h in range(2)])
-        ms.extend([sb(f"m{h}", [P, 2, S], F32) for h in range(2)])
-
-        def first_product(c):
-            xq = quantize(f"xq{c}", x_woven[c].rearrange("p r j -> p (r j)"), P, E4M3)
-            a = bank(f"A{c}", f"a{c}", [P, S])
-            nc.tensor.matmul_mx(out=a[:], lhsT=xq[0], lhsT_scale=xq[1], rhs=w1d[0], rhs_scale=w1d[1], start=True, stop=True)
-            return a
-
-        def form_z(c, a):
-            h, k = divmod(c, 2)
-            z = zzs[h][:, k, :]
-            nc.vector.scalar_tensor_tensor(out=z, in0=a[:], scalar=us_cols[:, c : c + 1], in1=ts_slots[:], op0=ALU.mult, op1=ALU.mult)
-            nc.scalar.activation(out=ths[h][:, k, :], in_=z, func=ACT.Tanh, scale=0.5)
-            nc.scalar.activation(out=ms[h][:, k, :], in_=z, func=ACT.Silu, scale=-1.0)
-
-        a0 = first_product(0)
-        x_last = sb("x_last", [P, P, PACK], BF16, "w1_plane3")
-        x_woven.append(x_last[:])
-        weave_rows(x_woven[3], x_halves, 3, nc.vector.tensor_copy)
-        turned1 = turned_half(1, tb, "xq0_codes")
-        a1 = first_product(1)
-        form_z(0, a0)
-        a3 = first_product(3)
-        a2 = first_product(2)
-        form_z(1, a1)
-        form_z(2, a2)
-        form_z(3, a3)
-
-        ts_twice = ts_slots[:].unsqueeze(1).to_broadcast([P, 2, S])
-
-        def first(h, t):
-            nc.vector.scalar_tensor_tensor(out=t, in0=ths[h][:], scalar=1.0, in1=ts_twice, op0=ALU.add, op1=ALU.mult)
-            tss.append(t)
-
-        def second(h, f):
-            nc.vector.scalar_tensor_tensor(out=f, in0=ms[h][:], scalar=1.0, in1=tss[h], op0=ALU.subtract, op1=ALU.mult)
-            fs.extend([f[:, 0, :], f[:, 1, :]])
-
-        w2_listed = sb("w2_listed", [P, PACK, S], BF16, "us_cols")
         for j in range(2):
-            nc.vector.tensor_copy(out=w2_listed[:, j, :], in_=w2_planes[j][:].indirect(offsets[:]))
-        for j in range(2, PACK):
+            nc.vector.tensor_copy(out=w1_pairs[0][:, j, :], in_=w1_planes[j][:].indirect(offsets[:]))
+        weave(nc.vector.tensor_copy, w1_woven, w1_pairs[0], slice(0, 4), slice(0, 2))
+        turned0 = turn(0, 7)
+        nc.vector.tensor_copy(out=w1_pairs[1][:, 0, :], in_=w1_planes[2][:].indirect(offsets[:]))
+        w1i = [quantize("w1i0", turned0[:], D // 2, E4M3)]
+        nc.vector.tensor_copy(out=w1_pairs[1][:, 1, 0:256], in_=w1_planes[3][:].indirect(offsets[:, 0:16]))
+        nc.scalar.activation(out=w1_pairs[1][:, 1, 256:512], in_=w1_planes[3][:].indirect(offsets[:, 16:32]), func=ACT.Copy)
+        weave(nc.vector.tensor_copy, w1_woven, w1_pairs[1], slice(0, 2), slice(2, 4))
+        weave(nc.scalar.copy, w1_woven, w1_pairs[1], slice(2, 4), slice(2, 4))
+        turned1 = turn(1, 4)
+        woven_flat = w1_woven[:].rearrange("p s j -> p (s j)")
+        w1d = [quantize(f"w1d{w}", woven_flat[:, cols(w, 1024)], 256, E4M3) for w in range(2)]
+        w1i.append(quantize("w1i1", turned1[:], D // 2, E4M3))
+
+        dy_woven = sb("dy_woven", [P, R, PACK], BF16, "w1_woven")
+        for h in range(2):
+            nc.gpsimd.tensor_scalar(
+                out=dy_woven[:, cols(h, 256), :], in0=dy_raw[:, :, cols(h, 256)].rearrange("p j r -> p r j"),
+                scalar1=1.0, scalar2=0.0, op0=ALU.mult, op1=ALU.add,
+            )
+
+        z = sb("z", [P, PACK, R], F32)
+        th = sb("th", [P, PACK, R], F32)
+        m = sb("m", [P, PACK, R], F32)
+        for t in range(PACK):
+            a = bank(t, f"a{t}", [P, R])
+            product(a[:], w1d[t // 2], cols(t % 2), xq, slice(0, R))
+            nc.vector.scalar_tensor_tensor(out=z[:, t, :], in0=a[:], scalar=ts_cols[:, t : t + 1], in1=us_row[:], op0=ALU.mult, op1=ALU.mult)
+            nc.scalar.activation(out=th[:, t, :], in_=z[:, t, :], func=ACT.Tanh, scale=0.5)
+            nc.scalar.activation(out=m[:, t, :], in_=z[:, t, :], func=ACT.Silu, scale=-1.0)
+
+        gate = sb("gate", [P, PACK, R], F32)
+        f = sb("f", [P, PACK, R], F32)
+
+        def form_gate(part):
+            nc.vector.scalar_tensor_tensor(out=gate[:, part, :], in0=th[:, part, :], scalar=1.0, in1=table[:, part, :], op0=ALU.add, op1=ALU.mult)
+
+        def form_f(part):
+            nc.vector.scalar_tensor_tensor(out=f[:, part, :], in0=m[:, part, :], scalar=1.0, in1=gate[:, part, :], op0=ALU.subtract, op1=ALU.mult)
+
+        w2_listed = sb("w2_listed", [P, PACK, S], BF16, "us_row")
+        nc.vector.tensor_copy(out=w2_listed[:, 0, :], in_=w2_planes[0][:].indirect(offsets[:]))
+        for j in range(1, PACK):
             nc.scalar.activation(out=w2_listed[:, j, :], in_=w2_planes[j][:].indirect(offsets[:]), func=ACT.Copy)
-        t0 = sb("t0", [P, 2, S], F32)
-        for k in range(2):
-            th_plus_one = sb(f"th_plus_one{k}", [P, S], F32)
-            nc.gpsimd.tensor_scalar(out=th_plus_one[:], in0=ths[0][:, k, :], scalar1=1.0, scalar2=1.0, op0=ALU.mult, op1=ALU.add)
-            nc.gpsimd.tensor_tensor(out=t0[:, k, :], in0=th_plus_one[:], in1=ts_slots[:], op=ALU.mult)
-        tss.append(t0[:])
-        first(1, sb("t1", [P, 2, S], F32)[:])
-        second(0, sb("f0", [P, 2, S], F32)[:])
+        form_gate(slice(0, 2))
+        dyq = quantize("dyq", dy_woven[:].rearrange("p r j -> p (r j)"), R, E5M2)
+        form_f(slice(0, 2))
+        for form in (form_gate, form_f):
+            for t in (2, 3):
+                form(slice(t, t + 1))
+
         w2_woven = sb("w2_woven", [P, S, PACK], BF16)
-        for copy, part in ((nc.vector.tensor_copy, slice(0, 96)), (nc.scalar.copy, slice(96, P))):
-            copy(
-                out=w2_woven[:].rearrange("p (w q e) j -> p q w e j", w=2, e=2)[:, part],
-                in_=w2_listed[:].rearrange("p j (q w e) -> p q w e j", w=2, e=2)[:, part],
-            )
-        late = sb("late", [P, 2 * S + CHUNKS], F32, "w2_plane3")
-        da_cols = late[:, 2 * S : 2 * S + CHUNKS]
-        nc.vector.scalar_tensor_tensor(out=da_cols, in0=turned[:, 0:CHUNKS], scalar=-0.5, in1=wt_cols[:], op0=ALU.mult, op1=ALU.mult)
-        dy_woven = sb("dy_woven", [P, R, PACK], BF16, "z1")
-        for c in range(CHUNKS):
-            weave_rows(dy_woven[:, c * P : (c + 1) * P, :], dy_halves, c)
+        weave(nc.vector.tensor_copy, w2_woven, w2_listed, slice(0, 2), slice(0, 4))
+        weave(nc.vector.tensor_copy, w2_woven, w2_listed, slice(2, 4), slice(0, 4), slice(0, 64))
+        weave(nc.scalar.copy, w2_woven, w2_listed, slice(2, 4), slice(0, 4), slice(64, P))
+        woven_flat = w2_woven[:].rearrange("p s j -> p (s j)")
+        w2e = [quantize(f"w2e{w}", woven_flat[:, cols(w, 1024)], 256, E4M3) for w in range(2)]
 
-        def quantize_dy(h, tag=None):
-            return quantize(f"dy{h}", dy_woven[:, 2 * h * P : 2 * (h + 1) * P, :].rearrange("p r j -> p (r j)"), 2 * P, E5M2, tag)
-
-        def second_one(k):
-            f = late[:, k * S : (k + 1) * S]
-            nc.vector.scalar_tensor_tensor(out=f, in0=ms[1][:, k, :], scalar=1.0, in1=tss[1][:, k, :], op0=ALU.subtract, op1=ALU.mult)
-            fs.append(f)
-
-        second_one(0)
-        w2e = quantize("w2e", w2_woven[:].rearrange("p s j -> p (s j)"), S, E4M3)
-        second_one(1)
-        dyqs = [quantize_dy(0)]
-        w1i.append(quantize("w1i1", turned1[:], D // 2, E4M3, "us_cols"))
-        dyqs.append(quantize_dy(1))
-
-        das = []
-        for c in range(CHUNKS):
-            dyq = dyqs[c // 2]
-            cols = slice((c % 2) * P, (c % 2 + 1) * P)
-            dh = bank(f"B{c}", f"dh{c}", [P, S])
-            nc.tensor.matmul_mx(
-                out=dh[:], lhsT=dyq[0][:, cols], lhsT_scale=dyq[1][:, cols], rhs=w2e[0], rhs_scale=w2e[1], start=True, stop=True
-            )
-            das.append(dh)
+        dhs = [bank(4 + c, f"dh{c}", [P, PACK, P]) for c in range(CHUNKS)]
+        for first in range(0, CHUNKS, 2):
+            for w in range(2):
+                for c in (first, first + 1):
+                    for e in range(2):
+                        product(dhs[c][:, 2 * w + e, :], w2e[w], cols(e), dyq, cols(c))
 
         def form_da(c):
-            if c == 0:
-                scaled = sb("dh0_scaled", [P, S], F32)
-                nc.scalar.activation(out=scaled[:], in_=das[c][:], func=ACT.Copy, scale=da_cols[:, c : c + 1])
-                da = sb(f"da{c}", [P, S], BF16, "z1")
-                nc.gpsimd.tensor_tensor(out=da[:], in0=scaled[:], in1=fs[c], op=ALU.mult)
-            else:
-                da = sb(f"da{c}", [P, S], BF16)
-                nc.vector.scalar_tensor_tensor(
-                    out=da[:], in0=das[c][:], scalar=da_cols[:, c : c + 1], in1=fs[c], op0=ALU.mult, op1=ALU.mult
-                )
-            words = da[:].bitcast(F32)
-            tb = bank(f"A{max(c, 1)}", f"da_turn{c}", [P, 2, P])
-            for u in range(2):
-                nc.tensor.transpose(tb[:, u, :], words[:, u * P : (u + 1) * P], ident[:])
-            woven = sb(f"da_woven{c}", [P, P * PACK], BF16)
-            nc.scalar.copy(out=woven[:].bitcast(F32).rearrange("q (r u) -> q r u", u=2), in_=tb[:].rearrange("q u r -> q r u"))
-            return woven
+            da = sb(f"da{c}", [P, P * PACK], BF16)
+            nc.vector.tensor_tensor(
+                out=da[:].rearrange("q (g i t) -> q g t i", i=4, t=PACK),
+                in0=dhs[c][:].rearrange("q t (g i) -> q g t i", i=4),
+                in1=f[:, :, cols(c)].rearrange("q t (g i) -> q g t i", i=4),
+                op=ALU.mult,
+            )
+            return da
 
-        def finish(c, woven):
-            daq = quantize(f"daq{c}", woven[:], P, E5M2)
-            acc = bank(f"B{c}", f"acc{c}", [P, D])
-            for b in range(2):
-                nc.tensor.matmul_mx(
-                    out=acc[:, b * 2 * P : (b + 1) * 2 * P], lhsT=daq[0], lhsT_scale=daq[1], rhs=w1i[b][0], rhs_scale=w1i[b][1], start=True, stop=True
-                )
-            return acc
-
-        def store(c, acc):
-            res = sb(f"res{c}", [P, D], F32, (None, "ident", "da_woven3", None)[c])
+        def finish(c, da):
+            daq = quantize(f"daq{c}", da[:], P, E5M2)
+            res = sb(f"res{c}", [P, D], F32)
             res_view = res[:].rearrange("r (p b j) -> r p b j", b=2, j=2)
-            acc_view = acc[:].rearrange("r (b p j) -> r p b j", b=2, j=2)
-            rows = slice(c * P, (c + 1) * P)
-            if c in (1, CHUNKS - 1):
-                for k, queue in enumerate((nc.sync, nc.sync)):
-                    (nc.scalar.copy if c == 1 else nc.vector.tensor_copy)(out=res_view[:, 64 * k : 64 * (k + 1)], in_=acc_view[:, 64 * k : 64 * (k + 1)])
-                    queue.dma_start(out[rows, 256 * k : 256 * (k + 1)], res[:, 256 * k : 256 * (k + 1)])
+            if c < CHUNKS - 1:
+                acc = bank(c, f"acc{c}", [P, D])
+                for b in range(2):
+                    product(acc[:, cols(b, 256)], daq, slice(0, P), w1i[b], slice(0, 256))
+                nc.scalar.copy(out=res_view, in_=acc[:].rearrange("r (b p j) -> r p b j", b=2, j=2))
+                nc.sync.dma_start(out[cols(c), :], res[:])
             else:
-                (nc.vector.tensor_copy if c == 2 else nc.scalar.copy)(out=res_view, in_=acc_view)
-                nc.sync.dma_start(out[rows, :], res[:])
+                for k, copy in enumerate((nc.scalar.copy, nc.vector.tensor_copy)):
+                    acc = bank(c + k, f"acc{c + k}", [P, D // 2])
+                    for b in range(2):
+                        product(acc[:, cols(b)], daq, slice(0, P), w1i[b], cols(k))
+                    copy(out=res_view[:, cols(k, 64)], in_=acc[:].rearrange("r (b p j) -> r p b j", b=2, j=2))
+                    nc.sync.dma_start(out[cols(c), cols(k, 256)], res[:, cols(k, 256)])
 
-        order = (1, 2, 0, 3)
-        wov = [form_da(c) for c in order]
-        accs = [finish(c, wov[k]) for k, c in enumerate(order)]
-        for k, c in enumerate(order):
-            store(c, accs[k])
+        das = [form_da(0)]
+        for c in range(CHUNKS):
+            if c + 1 < CHUNKS:
+                das.append(form_da(c + 1))
+            finish(c, das[c])

@@ -44,7 +44,7 @@ def tile_attend_gffn_sil_x_kernel(tc, xT, w1, dyT, w2, us, ts, wt, offs, out):
         w1_planes = [sb(f"w1_plane{j}", [P, T], F32) for j in range(PACK)]
         w2_planes = [sb(f"w2_plane{j}", [P, T], F32) for j in range(PACK)]
         x_raw = sb("x_raw", [P, PACK, R], F32)
-        dy_raw = sb("dy_raw", [P, PACK, R], F32)
+        dy_raw = at(4096, "dy_raw", [P, PACK, R], F32)
         us_cols = sb("us_cols", [P, PACK], F32)
         wt_cols = sb("wt_cols", [P, PACK], F32)
         ts_window = sb("ts_window", [P, T], F32)
@@ -68,8 +68,8 @@ def tile_attend_gffn_sil_x_kernel(tc, xT, w1, dyT, w2, us, ts, wt, offs, out):
         ident = sb("ident", [P, P], F32)
         make_identity(nc, ident[:])
 
-        def quantize(name, woven, width, fmt, tag=None):
-            codes = sb(name + "_codes", [P, width], U32, tag)
+        def quantize(name, woven, width, fmt, offset=None):
+            codes = sb(name + "_codes", [P, width], U32) if offset is None else at(offset, name + "_codes", [P, width], U32)
             scales = sb(name + "_scales", [P, width], U8)
             nc.vector.quantize_mx(out=codes[:].bitcast(fmt), scales=scales[:], in_=woven)
             return codes[:].bitcast(fmt), scales[:]
@@ -153,7 +153,6 @@ def tile_attend_gffn_sil_x_kernel(tc, xT, w1, dyT, w2, us, ts, wt, offs, out):
         turned1 = turn(1, 4)
         woven_flat = w1_woven[:].rearrange("p s j -> p (s j)")
         w1d = [quantize(f"w1d{w}", woven_flat[:, cols(w, 1024)], 256, E4M3) for w in range(2)]
-        w1i.append(quantize("w1i1", turned1[:], D // 2, E4M3))
 
         dy_woven = sb("dy_woven", [P, R, PACK], BF16, "w1_woven")
         for h in range(2):
@@ -172,7 +171,7 @@ def tile_attend_gffn_sil_x_kernel(tc, xT, w1, dyT, w2, us, ts, wt, offs, out):
             nc.scalar.activation(out=th[:, t, :], in_=z[:, t, :], func=ACT.Tanh, scale=0.5)
             nc.scalar.activation(out=m[:, t, :], in_=z[:, t, :], func=ACT.Silu, scale=-1.0)
 
-        gate = sb("gate", [P, PACK, R], F32)
+        gate = at(4096 + 1024, "gate", [P, PACK, R], F32)
         f = sb("f", [P, PACK, R], F32)
 
         def form_gate(part):
@@ -188,6 +187,7 @@ def tile_attend_gffn_sil_x_kernel(tc, xT, w1, dyT, w2, us, ts, wt, offs, out):
         form_gate(slice(0, 2))
         dyq = quantize("dyq", dy_woven[:].rearrange("p r j -> p (r j)"), R, E5M2)
         form_f(slice(0, 2))
+        w1i.append(quantize("w1i1", turned1[:], D // 2, E4M3, 4096))
         for form in (form_gate, form_f):
             for t in (2, 3):
                 form(slice(t, t + 1))

@@ -44,26 +44,26 @@ def tile_attend_gffn_sil_x_kernel(tc, xT, w1, dyT, w2, us, ts, wt, offs, out):
         w1_planes = [sb(f"w1_plane{j}", [P, T], F32) for j in range(PACK)]
         w2_planes = [sb(f"w2_plane{j}", [P, T], F32) for j in range(PACK)]
         x_raw = sb("x_raw", [P, PACK, R], F32)
-        dy_raw = at(4096, "dy_raw", [P, PACK, R], F32)
+        dy_raw = sb("dy_raw", [P, PACK, R], F32)
         us_cols = sb("us_cols", [P, PACK], F32)
         wt_cols = sb("wt_cols", [P, PACK], F32)
-        ts_window = sb("ts_window", [P, T], F32)
-
+        ts_window = at(16384, "ts_window", [P, T], F32)
         ts_pieces = sb("ts_pieces", [P, T // P], F32)
-        nc.scalar.dma_start(ts_pieces[:], ts[0:1, :].rearrange("o (p c) -> (o p) c", p=P))
-        nc.scalar.dma_start(us_cols[:], us.rearrange("(p c) o -> p (c o)", c=PACK))
-        nc.scalar.dma_start(wt_cols[:], wt.rearrange("(p c) o -> p (c o)", c=PACK))
+
         warm = sb("warm", [P, 2], F32)
         nc.gpsimd.memset(warm[:, 0:1], 0.0)
         nc.scalar.activation(out=warm[:, 1:2], in_=warm[:, 0:1], func=ACT.Silu)
 
+        nc.sync.dma_start(ts_pieces[:], ts[0:1, :].rearrange("o (p c) -> (o p) c", p=P))
         nc.sync.dma_start(x_raw[:], xT.rearrange("(p j) r -> p j r", j=PACK))
         nc.sync.dma_start(offsets[:], offs)
+        nc.sync.dma_start(us_cols[:], us.rearrange("(p c) o -> p (c o)", c=PACK))
+        nc.sync.dma_start(wt_cols[:], wt.rearrange("(p c) o -> p (c o)", c=PACK))
         for j in range(PACK):
             nc.sync.dma_start(w1_planes[j][:], w1_rows[:, j, :])
-        nc.sync.dma_start(dy_raw[:], dyT.rearrange("(p j) r -> p j r", j=PACK))
         for j in range(PACK):
             nc.sync.dma_start(w2_planes[j][:], w2_rows[:, j, :])
+        nc.sync.dma_start(dy_raw[:], dyT.rearrange("(p j) r -> p j r", j=PACK))
 
         ident = sb("ident", [P, P], F32)
         make_identity(nc, ident[:])
@@ -91,6 +91,9 @@ def tile_attend_gffn_sil_x_kernel(tc, xT, w1, dyT, w2, us, ts, wt, offs, out):
                 nc.tensor.transpose(spread[:, k, :], ts_pieces[:, c : c + 1].to_broadcast([P, P]), ident[:])
             nc.scalar.activation(out=ts_view[:, :, 4 * g : 4 * g + 4], in_=spread[:].rearrange("m k n -> m n k"), func=ACT.Copy)
 
+        ts_listed = at(2048, "ts_listed", [P, S], F32)
+        nc.scalar.activation(out=ts_listed[:], in_=ts_window[:].indirect(offsets[:]), func=ACT.Copy)
+
         c_cols = sb("c_cols", [P, PACK], F32)
         half_us = sb("half_us", [P, PACK], F32)
         nc.gpsimd.tensor_scalar(out=half_us[:], in0=us_cols[:], scalar1=-0.5, scalar2=0.0, op0=ALU.mult, op1=ALU.add)
@@ -100,34 +103,39 @@ def tile_attend_gffn_sil_x_kernel(tc, xT, w1, dyT, w2, us, ts, wt, offs, out):
         for spread, source in ((us_spread, us_cols), (c_spread, c_cols)):
             for c in range(PACK):
                 nc.tensor.transpose(spread[:, c, :], source[:, c : c + 1].to_broadcast([P, P]), ident[:])
-        us_row = sb("us_row", [P, R], F32)
+        us_row = at(16384, "us_row", [P, R], F32)
         nc.scalar.copy(out=us_row[:].rearrange("m (p c) -> m p c", c=PACK), in_=us_spread[:].rearrange("m c p -> m p c"))
-        c_row = sb("c_row", [P, R], F32)
+        c_row = at(16384 + 2048, "c_row", [P, R], F32)
         nc.scalar.copy(out=c_row[:].rearrange("m (p c) -> m p c", c=PACK), in_=c_spread[:].rearrange("m c p -> m p c"))
 
-        x_woven = sb("x_woven", [P, R, PACK], BF16)
-        nc.vector.tensor_copy(
-            out=x_woven[:].rearrange("p (g i) j -> p g j i", i=4), in_=x_raw[:].rearrange("p j (g i) -> p g j i", i=4)
-        )
-        ts_listed = at(2048, "ts_listed", [P, S], F32)
-        nc.scalar.activation(out=ts_listed[:], in_=ts_window[:].indirect(offsets[:]), func=ACT.Copy)
-        xq = quantize("xq", x_woven[:].rearrange("p r j -> p (r j)"), R, E4M3)
         ts_turn = bank(6, "ts_turn", [P, PACK, P])
         for t in range(PACK):
             nc.tensor.transpose(ts_turn[:, t, :], ts_listed[:, t : S : PACK], ident[:])
         ts_cols = sb("ts_cols", [P, PACK], F32)
+        ts_early = at(4096, "ts_early", [P, PACK - 1], F32)
         nc.scalar.copy(out=ts_cols[:], in_=ts_turn[:, :, 0])
-        table = sb("table", [P, PACK, R], F32)
-        for t in range(PACK):
-            nc.gpsimd.tensor_scalar(out=table[:, t, :], in0=c_row[:], scalar1=ts_cols[:, t : t + 1], scalar2=0.0, op0=ALU.mult, op1=ALU.add)
+        nc.scalar.copy(out=ts_early[:], in_=ts_turn[:, 0 : PACK - 1, 0])
+        tables = {2: at(24576 + 1024, "table2", [P, R], F32), 3: sb("table3", [P, R], F32)}
+        for t in (2, 3):
+            nc.gpsimd.tensor_scalar(out=tables[t][:], in0=c_row[:], scalar1=ts_cols[:, t : t + 1], scalar2=0.0, op0=ALU.mult, op1=ALU.add)
+
+        def weave_rows(copy, woven, raw, rows):
+            copy(
+                out=woven[:, rows, :].rearrange("p (g i) j -> p g j i", i=4),
+                in_=raw[:, :, rows].rearrange("p j (g i) -> p g j i", i=4),
+            )
+
+        x_woven = sb("x_woven", [P, R, PACK], BF16)
+        weave_rows(nc.vector.tensor_copy, x_woven, x_raw, slice(0, R))
+        xq = quantize("xq", x_woven[:].rearrange("p r j -> p (r j)"), R, E4M3)
 
         w1_pairs = [at(64 * u, f"w1_pair{u}", [P, 2, S], BF16) for u in range(2)]
         w1_woven = sb("w1_woven", [P, S, PACK], BF16)
 
-        def weave(copy, woven, listed, places, planes, part=slice(0, P)):
+        def weave_pair(copy, u, places):
             copy(
-                out=woven[:].rearrange("p (t q) j -> p q t j", t=PACK)[:, part, places, planes],
-                in_=listed[:].rearrange("p j (q t) -> p q t j", t=PACK)[:, part, places, :],
+                out=w1_woven[:].rearrange("p (t q) j -> p q t j", t=PACK)[:, :, places, 2 * u : 2 * u + 2],
+                in_=w1_pairs[u][:].rearrange("p j (q t) -> p q t j", t=PACK)[:, :, places, :],
             )
 
         def turn(b, number):
@@ -142,69 +150,76 @@ def tile_attend_gffn_sil_x_kernel(tc, xT, w1, dyT, w2, us, ts, wt, offs, out):
 
         for j in range(2):
             nc.vector.tensor_copy(out=w1_pairs[0][:, j, :], in_=w1_planes[j][:].indirect(offsets[:]))
-        weave(nc.vector.tensor_copy, w1_woven, w1_pairs[0], slice(0, 4), slice(0, 2))
-        turned0 = turn(0, 7)
+        weave_pair(nc.vector.tensor_copy, 0, slice(0, 4))
+        turned0 = turn(0, 6)
         nc.vector.tensor_copy(out=w1_pairs[1][:, 0, :], in_=w1_planes[2][:].indirect(offsets[:]))
         w1i = [quantize("w1i0", turned0[:], D // 2, E4M3)]
         nc.vector.tensor_copy(out=w1_pairs[1][:, 1, 0:256], in_=w1_planes[3][:].indirect(offsets[:, 0:16]))
         nc.scalar.activation(out=w1_pairs[1][:, 1, 256:512], in_=w1_planes[3][:].indirect(offsets[:, 16:32]), func=ACT.Copy)
-        weave(nc.vector.tensor_copy, w1_woven, w1_pairs[1], slice(0, 2), slice(2, 4))
-        weave(nc.scalar.copy, w1_woven, w1_pairs[1], slice(2, 4), slice(2, 4))
+        weave_pair(nc.vector.tensor_copy, 1, slice(0, 2))
+        weave_pair(nc.scalar.copy, 1, slice(2, 4))
         turned1 = turn(1, 4)
         woven_flat = w1_woven[:].rearrange("p s j -> p (s j)")
         w1d = [quantize(f"w1d{w}", woven_flat[:, cols(w, 1024)], 256, E4M3) for w in range(2)]
 
-        dy_woven = sb("dy_woven", [P, R, PACK], BF16, "w1_woven")
-        for h in range(2):
-            nc.gpsimd.tensor_scalar(
-                out=dy_woven[:, cols(h, 256), :], in0=dy_raw[:, :, cols(h, 256)].rearrange("p j r -> p r j"),
-                scalar1=1.0, scalar2=0.0, op0=ALU.mult, op1=ALU.add,
-            )
+        w1i.append(quantize("w1i1", turned1[:], D // 2, E4M3))
 
-        z = sb("z", [P, PACK, R], F32)
+        zs = [sb(f"z{t}", [P, R], F32) for t in range(PACK)]
         th = sb("th", [P, PACK, R], F32)
         m = sb("m", [P, PACK, R], F32)
+        gate = sb("gate", [P, PACK, R], F32)
+        f = at(24576, "f", [P, PACK, R], F32)
         for t in range(PACK):
             a = bank(t, f"a{t}", [P, R])
             product(a[:], w1d[t // 2], cols(t % 2), xq, slice(0, R))
-            nc.vector.scalar_tensor_tensor(out=z[:, t, :], in0=a[:], scalar=ts_cols[:, t : t + 1], in1=us_row[:], op0=ALU.mult, op1=ALU.mult)
-            nc.scalar.activation(out=th[:, t, :], in_=z[:, t, :], func=ACT.Tanh, scale=0.5)
-            nc.scalar.activation(out=m[:, t, :], in_=z[:, t, :], func=ACT.Silu, scale=-1.0)
+            nc.vector.scalar_tensor_tensor(out=zs[t][:], in0=a[:], scalar=ts_early[:, t : t + 1] if t < PACK - 1 else ts_cols[:, t : t + 1], in1=us_row[:], op0=ALU.mult, op1=ALU.mult)
+            nc.scalar.activation(out=th[:, t, :], in_=zs[t][:], func=ACT.Tanh, scale=0.5)
+            nc.scalar.activation(out=m[:, t, :], in_=zs[t][:], func=ACT.Silu, scale=-1.0)
+            if t < 2:
+                lifted = sb(f"lifted{t}", [P, R], F32)
+                nc.gpsimd.tensor_scalar(
+                    out=lifted[:], in0=th[:, t, :], scalar1=1.0, scalar2=ts_cols[:, t : t + 1], op0=ALU.add, op1=ALU.mult
+                )
+                nc.gpsimd.tensor_tensor(out=gate[:, t, :], in0=lifted[:], in1=c_row[:], op=ALU.mult)
 
-        gate = at(4096 + 1024, "gate", [P, PACK, R], F32)
-        f = sb("f", [P, PACK, R], F32)
-
-        def form_gate(part):
-            nc.vector.scalar_tensor_tensor(out=gate[:, part, :], in0=th[:, part, :], scalar=1.0, in1=table[:, part, :], op0=ALU.add, op1=ALU.mult)
-
-        def form_f(part):
-            nc.vector.scalar_tensor_tensor(out=f[:, part, :], in0=m[:, part, :], scalar=1.0, in1=gate[:, part, :], op0=ALU.subtract, op1=ALU.mult)
-
-        w2_listed = sb("w2_listed", [P, PACK, S], BF16, "us_row")
-        nc.vector.tensor_copy(out=w2_listed[:, 0, :], in_=w2_planes[0][:].indirect(offsets[:]))
-        for j in range(1, PACK):
+        w2_listed = at(4096, "w2_listed", [P, PACK, S], BF16)
+        for j in range(2):
+            nc.vector.tensor_copy(out=w2_listed[:, j, :], in_=w2_planes[j][:].indirect(offsets[:]))
+        for j in range(2, PACK):
             nc.scalar.activation(out=w2_listed[:, j, :], in_=w2_planes[j][:].indirect(offsets[:]), func=ACT.Copy)
-        form_gate(slice(0, 2))
-        dyq = quantize("dyq", dy_woven[:].rearrange("p r j -> p (r j)"), R, E5M2)
-        form_f(slice(0, 2))
-        w1i.append(quantize("w1i1", turned1[:], D // 2, E4M3, 4096))
-        for form in (form_gate, form_f):
-            for t in (2, 3):
-                form(slice(t, t + 1))
+        for t in (2, 3):
+            nc.vector.scalar_tensor_tensor(out=gate[:, t, :], in0=th[:, t, :], scalar=1.0, in1=tables[t][:], op0=ALU.add, op1=ALU.mult)
+        for part in (slice(0, 1), slice(2, 4), slice(1, 2)):
+            nc.vector.scalar_tensor_tensor(
+                out=f[:, part, :], in0=m[:, part, :], scalar=1.0, in1=gate[:, part, :], op0=ALU.subtract, op1=ALU.mult
+            )
 
         w2_woven = sb("w2_woven", [P, S, PACK], BF16)
-        weave(nc.vector.tensor_copy, w2_woven, w2_listed, slice(0, 2), slice(0, 4))
-        weave(nc.vector.tensor_copy, w2_woven, w2_listed, slice(2, 4), slice(0, 4), slice(0, 64))
-        weave(nc.scalar.copy, w2_woven, w2_listed, slice(2, 4), slice(0, 4), slice(64, P))
+
+        def weave_w2(copy, w, part):
+            copy(
+                out=w2_woven[:].rearrange("p (t g i) j -> p g t i j", t=PACK, i=2)[:, part, 2 * w : 2 * w + 2],
+                in_=w2_listed[:].rearrange("p j (g i t) -> p g t i j", t=PACK, i=2)[:, part, 2 * w : 2 * w + 2],
+            )
+
+        weave_w2(nc.vector.tensor_copy, 0, slice(0, 64))
+        weave_w2(nc.vector.tensor_copy, 1, slice(0, 24))
+        weave_w2(nc.scalar.copy, 1, slice(24, 64))
+        dy_woven = sb("dy_woven", [P, R, PACK], BF16, "w2_plane3")
+        for h in range(2):
+            weave_rows(nc.scalar.copy, dy_woven, dy_raw, cols(h, 256))
         woven_flat = w2_woven[:].rearrange("p s j -> p (s j)")
-        w2e = [quantize(f"w2e{w}", woven_flat[:, cols(w, 1024)], 256, E4M3) for w in range(2)]
+        dy_flat = dy_woven[:].rearrange("p r j -> p (r j)")
+        w2e = [quantize("w2e0", woven_flat[:, 0:1024], 256, E4M3)]
+        dyq = [quantize("dyq0", dy_flat[:, 0:1024], 256, E5M2, 4096 + 1024)]
+        w2e.append(quantize("w2e1", woven_flat[:, 1024:2048], 256, E4M3))
 
         dhs = [bank(4 + c, f"dh{c}", [P, PACK, P]) for c in range(CHUNKS)]
-        for first in range(0, CHUNKS, 2):
-            for w in range(2):
-                for c in (first, first + 1):
-                    for e in range(2):
-                        product(dhs[c][:, 2 * w + e, :], w2e[w], cols(e), dyq, cols(c))
+
+        for w in range(2):
+            for c in range(2):
+                for e in range(2):
+                    product(dhs[c][:, 2 * w + e, :], w2e[w], cols(e), dyq[0], cols(c))
 
         def form_da(c):
             da = sb(f"da{c}", [P, P * PACK], BF16)
@@ -235,6 +250,10 @@ def tile_attend_gffn_sil_x_kernel(tc, xT, w1, dyT, w2, us, ts, wt, offs, out):
                     nc.sync.dma_start(out[cols(c), cols(k, 256)], res[:, cols(k, 256)])
 
         das = [form_da(0)]
+        dyq.append(quantize("dyq1", dy_flat[:, 1024:2048], 256, E5M2, 4096 + 64))
+        for c in (2, 3):
+            for t in range(PACK):
+                product(dhs[c][:, t, :], w2e[t // 2], cols(t % 2), dyq[1], cols(c - 2))
         for c in range(CHUNKS):
             if c + 1 < CHUNKS:
                 das.append(form_da(c + 1))

@@ -45,11 +45,12 @@ def tile_attend_gffn_sil_x_kernel(tc, xT, w1, dyT, w2, us, ts, wt, offs, out):
         w2_planes = [sb(f"w2_plane{j}", [P, T], F32) for j in range(PACK)]
         x_raw = sb("x_raw", [P, PACK, R], F32)
         dy_raw = sb("dy_raw", [P, PACK, R], F32)
-        us_cols = sb("us_cols", [P, PACK], F32)
-        wt_cols = sb("wt_cols", [P, PACK], F32)
-        ts_window = at(16384, "ts_window", [P, T], F32)
         ts_pieces = sb("ts_pieces", [P, T // P], F32)
+        ts_window = sb("ts_window", [P, T], F32)
+        row_scales = sb("row_scales", [P, P], F32)
 
+        nc.gpsimd.memset(row_scales[:], 0.0)
+        scale_rows = sb("scale_rows", [2 * CHUNKS, P], F32)
         warm = sb("warm", [P, 2], F32)
         nc.gpsimd.memset(warm[:, 0:1], 0.0)
         nc.scalar.activation(out=warm[:, 1:2], in_=warm[:, 0:1], func=ACT.Silu)
@@ -57,8 +58,8 @@ def tile_attend_gffn_sil_x_kernel(tc, xT, w1, dyT, w2, us, ts, wt, offs, out):
         nc.sync.dma_start(ts_pieces[:], ts[0:1, :].rearrange("o (p c) -> (o p) c", p=P))
         nc.sync.dma_start(x_raw[:], xT.rearrange("(p j) r -> p j r", j=PACK))
         nc.sync.dma_start(offsets[:], offs)
-        nc.sync.dma_start(us_cols[:], us.rearrange("(p c) o -> p (c o)", c=PACK))
-        nc.sync.dma_start(wt_cols[:], wt.rearrange("(p c) o -> p (c o)", c=PACK))
+        nc.sync.dma_start(scale_rows[0:CHUNKS, :], us.rearrange("(c p) o -> c (p o)", p=P))
+        nc.sync.dma_start(scale_rows[CHUNKS : 2 * CHUNKS, :], wt.rearrange("(c p) o -> c (p o)", p=P))
         for j in range(PACK):
             nc.sync.dma_start(w1_planes[j][:], w1_rows[:, j, :])
         for j in range(PACK):
@@ -91,26 +92,33 @@ def tile_attend_gffn_sil_x_kernel(tc, xT, w1, dyT, w2, us, ts, wt, offs, out):
                 nc.tensor.transpose(spread[:, k, :], ts_pieces[:, c : c + 1].to_broadcast([P, P]), ident[:])
             nc.scalar.activation(out=ts_view[:, :, 4 * g : 4 * g + 4], in_=spread[:].rearrange("m k n -> m n k"), func=ACT.Copy)
 
-        ts_listed = at(2048, "ts_listed", [P, S], F32)
+        nc.gpsimd.tensor_copy(out=row_scales[0 : 2 * CHUNKS, :], in_=scale_rows[:])
+        turned_scales = bank(6, "turned_scales", [P, P])
+        nc.tensor.transpose(turned_scales[:], row_scales[:], ident[:])
+        scale_cols = sb("scale_cols", [P, 2 * CHUNKS], F32)
+        nc.scalar.copy(out=scale_cols[:], in_=turned_scales[:, 0 : 2 * CHUNKS])
+        c_cols = sb("c_cols", [P, CHUNKS], F32)
+        half_us = sb("half_us", [P, CHUNKS], F32)
+        nc.gpsimd.tensor_scalar(out=half_us[:], in0=scale_cols[:, 0:CHUNKS], scalar1=-0.5, scalar2=0.0, op0=ALU.mult, op1=ALU.add)
+        nc.gpsimd.tensor_tensor(out=c_cols[:], in0=half_us[:], in1=scale_cols[:, CHUNKS : 2 * CHUNKS], op=ALU.mult)
+        us_spread = bank(4, "us_spread", [P, R])
+        c_spread = bank(5, "c_spread", [P, R])
+        for spread, source in ((us_spread, scale_cols), (c_spread, c_cols)):
+            for c in range(CHUNKS):
+                nc.tensor.transpose(spread[:, cols(c)], source[:, c : c + 1].to_broadcast([P, P]), ident[:])
+        us_row = sb("us_row", [P, R], F32)
+        nc.scalar.copy(out=us_row[:], in_=us_spread[:])
+        c_row = sb("c_row", [P, R], F32)
+        nc.scalar.copy(out=c_row[:], in_=c_spread[:])
+
+        ts_listed = sb("ts_listed", [P, S], F32)
         nc.scalar.activation(out=ts_listed[:], in_=ts_window[:].indirect(offsets[:]), func=ACT.Copy)
-
-        c_cols = sb("c_cols", [P, PACK], F32)
-        half_us = sb("half_us", [P, PACK], F32)
-        nc.gpsimd.tensor_scalar(out=half_us[:], in0=us_cols[:], scalar1=-0.5, scalar2=0.0, op0=ALU.mult, op1=ALU.add)
-        nc.gpsimd.tensor_tensor(out=c_cols[:], in0=half_us[:], in1=wt_cols[:], op=ALU.mult)
-        us_spread = bank(4, "us_spread", [P, PACK, P])
-        c_spread = bank(5, "c_spread", [P, PACK, P])
-        for spread, source in ((us_spread, us_cols), (c_spread, c_cols)):
-            for c in range(PACK):
-                nc.tensor.transpose(spread[:, c, :], source[:, c : c + 1].to_broadcast([P, P]), ident[:])
-        us_row = at(16384, "us_row", [P, R], F32)
-        nc.scalar.copy(out=us_row[:].rearrange("m (p c) -> m p c", c=PACK), in_=us_spread[:].rearrange("m c p -> m p c"))
-        c_row = at(16384 + 2048, "c_row", [P, R], F32)
-        nc.scalar.copy(out=c_row[:].rearrange("m (p c) -> m p c", c=PACK), in_=c_spread[:].rearrange("m c p -> m p c"))
-
+        ts_dealt = at(2048, "ts_dealt", [P, PACK, P], F32)
+        nc.scalar.copy(out=ts_dealt[:], in_=ts_listed[:].rearrange("m (q t) -> m t q", t=PACK))
         ts_turn = bank(6, "ts_turn", [P, PACK, P])
         for t in range(PACK):
-            nc.tensor.transpose(ts_turn[:, t, :], ts_listed[:, t : S : PACK], ident[:])
+            nc.tensor.transpose(ts_turn[:, t, :], ts_dealt[:, t, :], ident[:])
+
         ts_cols = sb("ts_cols", [P, PACK], F32)
         ts_early = at(4096, "ts_early", [P, PACK - 1], F32)
         nc.scalar.copy(out=ts_cols[:], in_=ts_turn[:, :, 0])
@@ -162,7 +170,6 @@ def tile_attend_gffn_sil_x_kernel(tc, xT, w1, dyT, w2, us, ts, wt, offs, out):
         woven_flat = w1_woven[:].rearrange("p s j -> p (s j)")
         w1d = [quantize(f"w1d{w}", woven_flat[:, cols(w, 1024)], 256, E4M3) for w in range(2)]
 
-        w1i.append(quantize("w1i1", turned1[:], D // 2, E4M3))
 
         zs = [sb(f"z{t}", [P, R], F32) for t in range(PACK)]
         th = sb("th", [P, PACK, R], F32)
@@ -178,7 +185,7 @@ def tile_attend_gffn_sil_x_kernel(tc, xT, w1, dyT, w2, us, ts, wt, offs, out):
             if t < 2:
                 lifted = sb(f"lifted{t}", [P, R], F32)
                 nc.gpsimd.tensor_scalar(
-                    out=lifted[:], in0=th[:, t, :], scalar1=1.0, scalar2=ts_cols[:, t : t + 1], op0=ALU.add, op1=ALU.mult
+                    out=lifted[:], in0=th[:, t, :], scalar1=ts_cols[:, t : t + 1], scalar2=ts_cols[:, t : t + 1], op0=ALU.mult, op1=ALU.add
                 )
                 nc.gpsimd.tensor_tensor(out=gate[:, t, :], in0=lifted[:], in1=c_row[:], op=ALU.mult)
 
@@ -213,6 +220,7 @@ def tile_attend_gffn_sil_x_kernel(tc, xT, w1, dyT, w2, us, ts, wt, offs, out):
         w2e = [quantize("w2e0", woven_flat[:, 0:1024], 256, E4M3)]
         dyq = [quantize("dyq0", dy_flat[:, 0:1024], 256, E5M2, 4096 + 1024)]
         w2e.append(quantize("w2e1", woven_flat[:, 1024:2048], 256, E4M3))
+        w1i.append(quantize("w1i1", turned1[:], D // 2, E4M3, 4096 + 3072))
 
         dhs = [bank(4 + c, f"dh{c}", [P, PACK, P]) for c in range(CHUNKS)]
 

@@ -44,7 +44,8 @@ def tile_attend_gffn_sil_x_kernel(tc, xT, w1, dyT, w2, us, ts, wt, offs, out):
         w1_planes = [sb(f"w1_plane{j}", [P, T], F32) for j in range(PACK)]
         w2_planes = [sb(f"w2_plane{j}", [P, T], F32) for j in range(PACK)]
         x_raw = sb("x_raw", [P, PACK, R], F32)
-        dy_raw = sb("dy_raw", [P, PACK, R], F32)
+        dy_halves = [sb(f"dy_half{h}", [P, PACK, R // 2], F32) for h in range(2)]
+        dy_rows = dyT.rearrange("(p j) r -> p j r", j=PACK)
         ts_pieces = sb("ts_pieces", [P, T // P], F32)
         ts_window = sb("ts_window", [P, T], F32)
         row_scales = sb("row_scales", [P, P], F32)
@@ -62,9 +63,10 @@ def tile_attend_gffn_sil_x_kernel(tc, xT, w1, dyT, w2, us, ts, wt, offs, out):
         nc.sync.dma_start(scale_rows[CHUNKS : 2 * CHUNKS, :], wt.rearrange("(c p) o -> c (p o)", p=P))
         for j in range(PACK):
             nc.sync.dma_start(w1_planes[j][:], w1_rows[:, j, :])
+        nc.sync.dma_start(dy_halves[0][:], dy_rows[:, :, 0 : R // 2])
         for j in range(PACK):
             nc.sync.dma_start(w2_planes[j][:], w2_rows[:, j, :])
-        nc.sync.dma_start(dy_raw[:], dyT.rearrange("(p j) r -> p j r", j=PACK))
+        nc.sync.dma_start(dy_halves[1][:], dy_rows[:, :, R // 2 : R])
 
         ident = sb("ident", [P, P], F32)
         make_identity(nc, ident[:])
@@ -108,8 +110,6 @@ def tile_attend_gffn_sil_x_kernel(tc, xT, w1, dyT, w2, us, ts, wt, offs, out):
                 nc.tensor.transpose(spread[:, cols(c)], source[:, c : c + 1].to_broadcast([P, P]), ident[:])
         us_row = sb("us_row", [P, R], F32)
         nc.scalar.copy(out=us_row[:], in_=us_spread[:])
-        c_row = sb("c_row", [P, R], F32)
-        nc.scalar.copy(out=c_row[:], in_=c_spread[:])
 
         ts_listed = sb("ts_listed", [P, S], F32)
         nc.scalar.activation(out=ts_listed[:], in_=ts_window[:].indirect(offsets[:]), func=ACT.Copy)
@@ -123,9 +123,9 @@ def tile_attend_gffn_sil_x_kernel(tc, xT, w1, dyT, w2, us, ts, wt, offs, out):
         ts_early = at(4096, "ts_early", [P, PACK - 1], F32)
         nc.scalar.copy(out=ts_cols[:], in_=ts_turn[:, :, 0])
         nc.scalar.copy(out=ts_early[:], in_=ts_turn[:, 0 : PACK - 1, 0])
-        tables = {2: at(24576 + 1024, "table2", [P, R], F32), 3: sb("table3", [P, R], F32)}
-        for t in (2, 3):
-            nc.gpsimd.tensor_scalar(out=tables[t][:], in0=c_row[:], scalar1=ts_cols[:, t : t + 1], scalar2=0.0, op0=ALU.mult, op1=ALU.add)
+        table = sb("table", [P, PACK, R], F32)
+        for t in range(PACK):
+            nc.scalar.activation(out=table[:, t, :], in_=c_spread[:], func=ACT.Copy, scale=ts_cols[:, t : t + 1])
 
         def weave_rows(copy, woven, raw, rows):
             copy(
@@ -142,8 +142,8 @@ def tile_attend_gffn_sil_x_kernel(tc, xT, w1, dyT, w2, us, ts, wt, offs, out):
 
         def weave_pair(copy, u, places):
             copy(
-                out=w1_woven[:].rearrange("p (t q) j -> p q t j", t=PACK)[:, :, places, 2 * u : 2 * u + 2],
-                in_=w1_pairs[u][:].rearrange("p j (q t) -> p q t j", t=PACK)[:, :, places, :],
+                out=w1_woven[:].rearrange("p (t g i) j -> p g t i j", t=PACK, i=2)[:, :, places, :, 2 * u : 2 * u + 2],
+                in_=w1_pairs[u][:].rearrange("p j (g i t) -> p g t i j", t=PACK, i=2)[:, :, places],
             )
 
         def turn(b, number):
@@ -152,54 +152,69 @@ def tile_attend_gffn_sil_x_kernel(tc, xT, w1, dyT, w2, us, ts, wt, offs, out):
             for jj in range(2):
                 for u in range(2):
                     nc.tensor.transpose(tb[:, 2 * jj + u, :], words[:, 256 * jj + u : 256 * (jj + 1) : 2], ident[:])
-            turned = sb(f"w1_turned{b}", [P, D // 2 * PACK], BF16)
+            return tb
+
+        def copy_turned(b, tb, tag=None):
+            turned = sb(f"w1_turned{b}", [P, D // 2 * PACK], BF16, tag)
             nc.scalar.copy(out=turned[:].bitcast(F32).rearrange("q (p k) -> q p k", k=4), in_=tb[:].rearrange("q k p -> q p k"))
             return turned
 
         for j in range(2):
             nc.vector.tensor_copy(out=w1_pairs[0][:, j, :], in_=w1_planes[j][:].indirect(offsets[:]))
         weave_pair(nc.vector.tensor_copy, 0, slice(0, 4))
-        turned0 = turn(0, 6)
+        turned0 = copy_turned(0, turn(0, 6))
         nc.vector.tensor_copy(out=w1_pairs[1][:, 0, :], in_=w1_planes[2][:].indirect(offsets[:]))
         w1i = [quantize("w1i0", turned0[:], D // 2, E4M3)]
         nc.vector.tensor_copy(out=w1_pairs[1][:, 1, 0:256], in_=w1_planes[3][:].indirect(offsets[:, 0:16]))
         nc.scalar.activation(out=w1_pairs[1][:, 1, 256:512], in_=w1_planes[3][:].indirect(offsets[:, 16:32]), func=ACT.Copy)
-        weave_pair(nc.vector.tensor_copy, 1, slice(0, 2))
+        for t in range(2):
+            weave_pair(nc.vector.tensor_copy, 1, slice(t, t + 1))
         weave_pair(nc.scalar.copy, 1, slice(2, 4))
-        turned1 = turn(1, 4)
         woven_flat = w1_woven[:].rearrange("p s j -> p (s j)")
-        w1d = [quantize(f"w1d{w}", woven_flat[:, cols(w, 1024)], 256, E4M3) for w in range(2)]
+        w1d = [quantize(f"w1d{t}", woven_flat[:, cols(t, 512)], P, E4M3) for t in range(2)]
+        w1d_late = quantize("w1d_late", woven_flat[:, 1024:2048], 256, E4M3)
 
+        dy_first = sb("dy_first", [P, R // 2, PACK], BF16, "w1_woven")
+        nc.gpsimd.tensor_scalar(
+            out=dy_first[:], in0=dy_halves[0][:].rearrange("p j r -> p r j"), scalar1=1.0, scalar2=0.0, op0=ALU.mult, op1=ALU.add
+        )
 
-        zs = [sb(f"z{t}", [P, R], F32) for t in range(PACK)]
+        z = sb("z", [P, PACK, R], F32)
         th = sb("th", [P, PACK, R], F32)
         m = sb("m", [P, PACK, R], F32)
-        gate = sb("gate", [P, PACK, R], F32)
-        f = at(24576, "f", [P, PACK, R], F32)
         for t in range(PACK):
             a = bank(t, f"a{t}", [P, R])
-            product(a[:], w1d[t // 2], cols(t % 2), xq, slice(0, R))
-            nc.vector.scalar_tensor_tensor(out=zs[t][:], in0=a[:], scalar=ts_early[:, t : t + 1] if t < PACK - 1 else ts_cols[:, t : t + 1], in1=us_row[:], op0=ALU.mult, op1=ALU.mult)
-            nc.scalar.activation(out=th[:, t, :], in_=zs[t][:], func=ACT.Tanh, scale=0.5)
-            nc.scalar.activation(out=m[:, t, :], in_=zs[t][:], func=ACT.Silu, scale=-1.0)
             if t < 2:
-                lifted = sb(f"lifted{t}", [P, R], F32)
-                nc.gpsimd.tensor_scalar(
-                    out=lifted[:], in0=th[:, t, :], scalar1=ts_cols[:, t : t + 1], scalar2=ts_cols[:, t : t + 1], op0=ALU.mult, op1=ALU.add
-                )
-                nc.gpsimd.tensor_tensor(out=gate[:, t, :], in0=lifted[:], in1=c_row[:], op=ALU.mult)
+                product(a[:], w1d[t], slice(0, P), xq, slice(0, R))
+            else:
+                product(a[:], w1d_late, cols(t - 2), xq, slice(0, R))
+            scale = (ts_early if t < PACK - 1 else ts_cols)[:, t : t + 1]
+            nc.vector.scalar_tensor_tensor(out=z[:, t, :], in0=a[:], scalar=scale, in1=us_row[:], op0=ALU.mult, op1=ALU.mult)
+            nc.scalar.activation(out=th[:, t, :], in_=z[:, t, :], func=ACT.Tanh, scale=0.5)
+            nc.scalar.activation(out=m[:, t, :], in_=z[:, t, :], func=ACT.Silu, scale=-1.0)
+        turn1 = turn(1, 0)
+
+        gate = sb("gate", [P, PACK, R], F32)
+        f = sb("f", [P, PACK, R], F32)
+
+        def form_gate(part):
+            nc.vector.scalar_tensor_tensor(out=gate[:, part, :], in0=th[:, part, :], scalar=1.0, in1=table[:, part, :], op0=ALU.add, op1=ALU.mult)
+
+        def form_f(part):
+            nc.vector.scalar_tensor_tensor(out=f[:, part, :], in0=m[:, part, :], scalar=1.0, in1=gate[:, part, :], op0=ALU.subtract, op1=ALU.mult)
 
         w2_listed = at(4096, "w2_listed", [P, PACK, S], BF16)
-        for j in range(2):
-            nc.vector.tensor_copy(out=w2_listed[:, j, :], in_=w2_planes[j][:].indirect(offsets[:]))
+        nc.vector.tensor_copy(out=w2_listed[:, 0, :], in_=w2_planes[0][:].indirect(offsets[:]))
+        nc.vector.tensor_copy(out=w2_listed[:, 1, 0:128], in_=w2_planes[1][:].indirect(offsets[:, 0:8]))
+        nc.scalar.activation(out=w2_listed[:, 1, 128:S], in_=w2_planes[1][:].indirect(offsets[:, 8:32]), func=ACT.Copy)
         for j in range(2, PACK):
             nc.scalar.activation(out=w2_listed[:, j, :], in_=w2_planes[j][:].indirect(offsets[:]), func=ACT.Copy)
-        for t in (2, 3):
-            nc.vector.scalar_tensor_tensor(out=gate[:, t, :], in0=th[:, t, :], scalar=1.0, in1=tables[t][:], op0=ALU.add, op1=ALU.mult)
-        for part in (slice(0, 1), slice(2, 4), slice(1, 2)):
-            nc.vector.scalar_tensor_tensor(
-                out=f[:, part, :], in0=m[:, part, :], scalar=1.0, in1=gate[:, part, :], op0=ALU.subtract, op1=ALU.mult
-            )
+        form_gate(slice(0, 2))
+        dyq = [quantize("dyq0", dy_first[:].rearrange("p r j -> p (r j)"), R // 2, E5M2)]
+        form_f(slice(0, 2))
+        for form in (form_gate, form_f):
+            for t in (2, 3):
+                form(slice(t, t + 1))
 
         w2_woven = sb("w2_woven", [P, S, PACK], BF16)
 
@@ -210,59 +225,66 @@ def tile_attend_gffn_sil_x_kernel(tc, xT, w1, dyT, w2, us, ts, wt, offs, out):
             )
 
         weave_w2(nc.vector.tensor_copy, 0, slice(0, 64))
-        weave_w2(nc.vector.tensor_copy, 1, slice(0, 24))
-        weave_w2(nc.scalar.copy, 1, slice(24, 64))
-        dy_woven = sb("dy_woven", [P, R, PACK], BF16, "w2_plane3")
-        for h in range(2):
-            weave_rows(nc.scalar.copy, dy_woven, dy_raw, cols(h, 256))
+        weave_w2(nc.vector.tensor_copy, 1, slice(0, 32))
+        weave_w2(nc.scalar.copy, 1, slice(32, 64))
+        dy_second = sb("dy_second", [P, R // 2, PACK], BF16, "w2_plane3")
+        nc.scalar.copy(
+            out=dy_second[:].rearrange("p (g i) j -> p g j i", i=4), in_=dy_halves[1][:].rearrange("p j (g i) -> p g j i", i=4)
+        )
         woven_flat = w2_woven[:].rearrange("p s j -> p (s j)")
-        dy_flat = dy_woven[:].rearrange("p r j -> p (r j)")
-        w2e = [quantize("w2e0", woven_flat[:, 0:1024], 256, E4M3)]
-        dyq = [quantize("dyq0", dy_flat[:, 0:1024], 256, E5M2, 4096 + 1024)]
-        w2e.append(quantize("w2e1", woven_flat[:, 1024:2048], 256, E4M3))
-        w1i.append(quantize("w1i1", turned1[:], D // 2, E4M3, 4096 + 3072))
+        w2e = [quantize(f"w2e{w}", woven_flat[:, cols(w, 1024)], 256, E4M3) for w in range(2)]
+        dyq.append(quantize("dyq1", dy_second[:].rearrange("p r j -> p (r j)"), R // 2, E5M2, 4096))
+        turned1 = copy_turned(1, turn1, "w2_plane3")
 
-        dhs = [bank(4 + c, f"dh{c}", [P, PACK, P]) for c in range(CHUNKS)]
-
-        for w in range(2):
-            for c in range(2):
+        half = R // 2
+        dhs = [[bank(4 + 2 * h + w, f"dh{h}{w}", [P, 2, half]) for w in range(2)] for h in range(2)]
+        for h in range(2):
+            for w in range(2):
                 for e in range(2):
-                    product(dhs[c][:, 2 * w + e, :], w2e[w], cols(e), dyq[0], cols(c))
+                    product(dhs[h][w][:, e, :], w2e[w], cols(e), dyq[h], slice(0, half))
 
-        def form_da(c):
-            da = sb(f"da{c}", [P, P * PACK], BF16)
+        def form_da(target, w, first, count):
+            h, start = divmod(first, half)
             nc.vector.tensor_tensor(
-                out=da[:].rearrange("q (g i t) -> q g t i", i=4, t=PACK),
-                in0=dhs[c][:].rearrange("q t (g i) -> q g t i", i=4),
-                in1=f[:, :, cols(c)].rearrange("q t (g i) -> q g t i", i=4),
+                out=target.rearrange("q (g i) e -> q g e i", i=4),
+                in0=dhs[h][w][:, :, start : start + count].rearrange("q e (g i) -> q g e i", i=4),
+                in1=f[:, 2 * w : 2 * w + 2, first : first + count].rearrange("q e (g i) -> q g e i", i=4),
                 op=ALU.mult,
             )
-            return da
 
-        def finish(c, da):
-            daq = quantize(f"daq{c}", da[:], P, E5M2)
+        def form_in_pairs(name, first, count):
+            pairs = sb(name + "_pairs", [P, 2, count * 2], BF16)
+            for w in range(2):
+                form_da(pairs[:, w, :].rearrange("q (r e) -> q r e", e=2), w, first, count)
+            woven = sb(name + "_woven", [P, count * PACK], BF16)
+            nc.scalar.copy(
+                out=woven[:].bitcast(F32).rearrange("q (r w) -> q r w", w=2), in_=pairs[:].bitcast(F32).rearrange("q w r -> q r w")
+            )
+            return woven
+
+        def finish(c, woven):
+            daq = quantize(f"daq{c}", woven, P, E5M2)
+            acc = bank(c, f"acc{c}", [P, D])
+            for b in range(2):
+                product(acc[:, cols(b, 256)], daq, slice(0, P), w1i[b], slice(0, 256))
             res = sb(f"res{c}", [P, D], F32)
             res_view = res[:].rearrange("r (p b j) -> r p b j", b=2, j=2)
+            acc_view = acc[:].rearrange("r (b p j) -> r p b j", b=2, j=2)
             if c < CHUNKS - 1:
-                acc = bank(c, f"acc{c}", [P, D])
-                for b in range(2):
-                    product(acc[:, cols(b, 256)], daq, slice(0, P), w1i[b], slice(0, 256))
-                nc.scalar.copy(out=res_view, in_=acc[:].rearrange("r (b p j) -> r p b j", b=2, j=2))
+                nc.scalar.copy(out=res_view, in_=acc_view)
                 nc.sync.dma_start(out[cols(c), :], res[:])
             else:
-                for k, copy in enumerate((nc.scalar.copy, nc.vector.tensor_copy)):
-                    acc = bank(c + k, f"acc{c + k}", [P, D // 2])
-                    for b in range(2):
-                        product(acc[:, cols(b)], daq, slice(0, P), w1i[b], cols(k))
-                    copy(out=res_view[:, cols(k, 64)], in_=acc[:].rearrange("r (b p j) -> r p b j", b=2, j=2))
+                for k in range(2):
+                    nc.vector.tensor_copy(out=res_view[:, cols(k, 64)], in_=acc_view[:, cols(k, 64)])
                     nc.sync.dma_start(out[cols(c), cols(k, 256)], res[:, cols(k, 256)])
 
-        das = [form_da(0)]
-        dyq.append(quantize("dyq1", dy_flat[:, 1024:2048], 256, E5M2, 4096 + 64))
-        for c in (2, 3):
-            for t in range(PACK):
-                product(dhs[c][:, t, :], w2e[t // 2], cols(t % 2), dyq[1], cols(c - 2))
-        for c in range(CHUNKS):
-            if c + 1 < CHUNKS:
-                das.append(form_da(c + 1))
-            finish(c, das[c])
+        das = [form_in_pairs(f"da{c}", c * P, P) for c in range(2)]
+        w1i.append(quantize("w1i1", turned1[:], D // 2, E4M3))
+        finish(0, das[0][:])
+        das.append(form_in_pairs("da2", 2 * P, P))
+        finish(1, das[1][:])
+        da_last = sb("da_last", [P, P, PACK], BF16)
+        for w in range(2):
+            form_da(da_last[:, :, 2 * w : 2 * w + 2], w, R - P, P)
+        finish(2, das[2][:])
+        finish(3, da_last[:].rearrange("q r t -> q (r t)"))

from contextlib import ExitStack

import concourse.mybir as mybir
from concourse.masks import make_identity

D, E, R, T, S = 512, 512, 512, 2048, 512
FLOPS = 3 * 2 * 512 * 512 * 512

F32 = mybir.dt.float32
BF16 = mybir.dt.bfloat16
U32 = mybir.dt.uint32
U16 = mybir.dt.uint16
U8 = mybir.dt.uint8
E4M3 = mybir.dt.float8_e4m3fn_x4
E5M2 = mybir.dt.float8_e5m2_x4
ACT = mybir.ActivationFunctionType
ALU = mybir.AluOpType

P = 128
PACK = 4
CHUNKS = R // P


def tile_attend_gffn_sil_x_kernel(tc, xT, w1, dyT, w2, us, ts, wt, offs, out):
    nc = tc.nc
    with ExitStack() as ctx:
        keep = ctx.enter_context(tc.tile_pool(name="keep", bufs=1))
        psum = ctx.enter_context(tc.psum_pool(name="psum", bufs=1))

        def sb(name, shape, dtype, tag=None):
            return keep.tile(shape, dtype, name=name, tag=tag or name, align_bytes=64)

        placed = ctx.enter_context(tc.tile_pool(name="placed", bufs=1))

        def at(offset, name, shape, dtype):
            return placed.tile(shape, dtype, name=name, align_bytes=64, offset=offset)

        def bank(number, name, shape):
            return psum.tile(shape, F32, name=name, tag=f"bank{number}")

        offsets = sb("offsets", [P, S // 16], U16)
        w1_rows = w1.rearrange("(p j) t -> p j t", j=PACK)
        w2_rows = w2.rearrange("(p j) t -> p j t", j=PACK)
        w1_planes = [sb(f"w1_plane{j}", [P, T], F32) for j in range(PACK)]
        w2_planes = [sb(f"w2_plane{j}", [P, T], F32) for j in range(PACK)]
        x_raw = sb("x_raw", [P, PACK, R], F32)
        dy_halves = [sb(f"dy_half{h}", [P, PACK, R // 2], F32) for h in range(2)]
        dy_rows = dyT.rearrange("(p j) r -> p j r", j=PACK)
        ts_pieces = sb("ts_pieces", [P, T // P], F32)
        ts_window = sb("ts_window", [P, T], F32)
        row_scales = sb("row_scales", [P, P], F32)

        nc.gpsimd.memset(row_scales[:], 0.0)
        scale_rows = sb("scale_rows", [2 * CHUNKS, P], F32)
        warm = sb("warm", [P, 2], F32)
        nc.gpsimd.memset(warm[:, 0:1], 0.0)
        nc.scalar.activation(out=warm[:, 1:2], in_=warm[:, 0:1], func=ACT.Silu)

        nc.sync.dma_start(ts_pieces[:], ts[0:1, :].rearrange("o (p c) -> (o p) c", p=P))
        nc.sync.dma_start(x_raw[:], xT.rearrange("(p j) r -> p j r", j=PACK))
        nc.sync.dma_start(offsets[:], offs)
        nc.sync.dma_start(scale_rows[0:CHUNKS, :], us.rearrange("(c p) o -> c (p o)", p=P))
        nc.sync.dma_start(scale_rows[CHUNKS : 2 * CHUNKS, :], wt.rearrange("(c p) o -> c (p o)", p=P))
        for j in range(PACK):
            nc.sync.dma_start(w1_planes[j][:], w1_rows[:, j, :])
        nc.sync.dma_start(dy_halves[0][:], dy_rows[:, :, 0 : R // 2])
        for j in range(PACK):
            nc.sync.dma_start(w2_planes[j][:], w2_rows[:, j, :])
        nc.sync.dma_start(dy_halves[1][:], dy_rows[:, :, R // 2 : R])

        ident = sb("ident", [P, P], F32)
        make_identity(nc, ident[:])

        def quantize(name, woven, width, fmt, offset=None):
            codes = sb(name + "_codes", [P, width], U32) if offset is None else at(offset, name + "_codes", [P, width], U32)
            scales = sb(name + "_scales", [P, width], U8)
            nc.vector.quantize_mx(out=codes[:].bitcast(fmt), scales=scales[:], in_=woven)
            return codes[:].bitcast(fmt), scales[:]

        def product(acc, stationary, s_cols, moving, m_cols):
            nc.tensor.matmul_mx(
                out=acc, lhsT=stationary[0][:, s_cols], lhsT_scale=stationary[1][:, s_cols],
                rhs=moving[0][:, m_cols], rhs_scale=moving[1][:, m_cols], start=True, stop=True,
            )

        def cols(k, width=P):
            return slice(k * width, (k + 1) * width)

        ts_view = ts_window[:].rearrange("m (n c) -> m n c", c=T // P)
        for g in range(4):
            spread = bank(g, f"spread{g}", [P, 4, P])
            for k in range(4):
                c = 4 * g + k
                nc.tensor.transpose(spread[:, k, :], ts_pieces[:, c : c + 1].to_broadcast([P, P]), ident[:])
            nc.scalar.activation(out=ts_view[:, :, 4 * g : 4 * g + 4], in_=spread[:].rearrange("m k n -> m n k"), func=ACT.Copy)

        nc.gpsimd.tensor_copy(out=row_scales[0 : 2 * CHUNKS, :], in_=scale_rows[:])
        turned_scales = bank(6, "turned_scales", [P, P])
        nc.tensor.transpose(turned_scales[:], row_scales[:], ident[:])
        scale_cols = sb("scale_cols", [P, 2 * CHUNKS], F32)
        nc.scalar.copy(out=scale_cols[:], in_=turned_scales[:, 0 : 2 * CHUNKS])
        c_cols = sb("c_cols", [P, CHUNKS], F32)
        half_us = sb("half_us", [P, CHUNKS], F32)
        nc.gpsimd.tensor_scalar(out=half_us[:], in0=scale_cols[:, 0:CHUNKS], scalar1=-0.5, scalar2=0.0, op0=ALU.mult, op1=ALU.add)
        nc.gpsimd.tensor_tensor(out=c_cols[:], in0=half_us[:], in1=scale_cols[:, CHUNKS : 2 * CHUNKS], op=ALU.mult)
        us_spread = bank(4, "us_spread", [P, R])
        c_spread = bank(5, "c_spread", [P, R])
        for spread, source in ((us_spread, scale_cols), (c_spread, c_cols)):
            for c in range(CHUNKS):
                nc.tensor.transpose(spread[:, cols(c)], source[:, c : c + 1].to_broadcast([P, P]), ident[:])
        us_row = sb("us_row", [P, R], F32)
        nc.scalar.copy(out=us_row[:], in_=us_spread[:])

        ts_listed = sb("ts_listed", [P, S], F32)
        nc.scalar.activation(out=ts_listed[:], in_=ts_window[:].indirect(offsets[:]), func=ACT.Copy)
        ts_dealt = at(2048, "ts_dealt", [P, PACK, P], F32)
        nc.scalar.copy(out=ts_dealt[:], in_=ts_listed[:].rearrange("m (q t) -> m t q", t=PACK))
        ts_turn = bank(6, "ts_turn", [P, PACK, P])
        for t in range(PACK):
            nc.tensor.transpose(ts_turn[:, t, :], ts_dealt[:, t, :], ident[:])

        ts_cols = sb("ts_cols", [P, PACK], F32)
        ts_early = at(4096, "ts_early", [P, PACK - 1], F32)
        nc.scalar.copy(out=ts_cols[:], in_=ts_turn[:, :, 0])
        nc.scalar.copy(out=ts_early[:], in_=ts_turn[:, 0 : PACK - 1, 0])
        table = sb("table", [P, PACK, R], F32)
        for t in range(PACK):
            nc.scalar.activation(out=table[:, t, :], in_=c_spread[:], func=ACT.Copy, scale=ts_cols[:, t : t + 1])

        def weave_rows(copy, woven, raw, rows):
            copy(
                out=woven[:, rows, :].rearrange("p (g i) j -> p g j i", i=4),
                in_=raw[:, :, rows].rearrange("p j (g i) -> p g j i", i=4),
            )

        x_woven = sb("x_woven", [P, R, PACK], BF16)
        weave_rows(nc.vector.tensor_copy, x_woven, x_raw, slice(0, R))
        xq = quantize("xq", x_woven[:].rearrange("p r j -> p (r j)"), R, E4M3)

        w1_pairs = [at(64 * u, f"w1_pair{u}", [P, 2, S], BF16) for u in range(2)]
        w1_woven = sb("w1_woven", [P, S, PACK], BF16)

        def weave_pair(copy, u, places):
            copy(
                out=w1_woven[:].rearrange("p (t g i) j -> p g t i j", t=PACK, i=2)[:, :, places, :, 2 * u : 2 * u + 2],
                in_=w1_pairs[u][:].rearrange("p j (g i t) -> p g t i j", t=PACK, i=2)[:, :, places],
            )

        def turn(b, number):
            words = w1_pairs[b][:].rearrange("p j s -> p (j s)").bitcast(F32)
            tb = bank(number, f"w1_turn{b}", [P, 4, P])
            for jj in range(2):
                for u in range(2):
                    nc.tensor.transpose(tb[:, 2 * jj + u, :], words[:, 256 * jj + u : 256 * (jj + 1) : 2], ident[:])
            return tb

        def copy_turned(b, tb, tag=None):
            turned = sb(f"w1_turned{b}", [P, D // 2 * PACK], BF16, tag)
            nc.scalar.copy(out=turned[:].bitcast(F32).rearrange("q (p k) -> q p k", k=4), in_=tb[:].rearrange("q k p -> q p k"))
            return turned

        for j in range(2):
            nc.vector.tensor_copy(out=w1_pairs[0][:, j, :], in_=w1_planes[j][:].indirect(offsets[:]))
        weave_pair(nc.vector.tensor_copy, 0, slice(0, 4))
        turned0 = copy_turned(0, turn(0, 6))
        nc.vector.tensor_copy(out=w1_pairs[1][:, 0, :], in_=w1_planes[2][:].indirect(offsets[:]))
        w1i = [quantize("w1i0", turned0[:], D // 2, E4M3)]
        nc.vector.tensor_copy(out=w1_pairs[1][:, 1, 0:256], in_=w1_planes[3][:].indirect(offsets[:, 0:16]))
        nc.scalar.activation(out=w1_pairs[1][:, 1, 256:512], in_=w1_planes[3][:].indirect(offsets[:, 16:32]), func=ACT.Copy)
        for t in range(2):
            weave_pair(nc.vector.tensor_copy, 1, slice(t, t + 1))
        weave_pair(nc.scalar.copy, 1, slice(2, 4))
        woven_flat = w1_woven[:].rearrange("p s j -> p (s j)")
        w1d = [quantize(f"w1d{t}", woven_flat[:, cols(t, 512)], P, E4M3) for t in range(2)]
        w1d_late = quantize("w1d_late", woven_flat[:, 1024:2048], 256, E4M3)

        dy_first = sb("dy_first", [P, R // 2, PACK], BF16, "w1_woven")
        nc.gpsimd.tensor_scalar(
            out=dy_first[:], in0=dy_halves[0][:].rearrange("p j r -> p r j"), scalar1=1.0, scalar2=0.0, op0=ALU.mult, op1=ALU.add
        )

        z = sb("z", [P, PACK, R], F32)
        th = sb("th", [P, PACK, R], F32)
        m = sb("m", [P, PACK, R], F32)
        for t in range(PACK):
            a = bank(t, f"a{t}", [P, R])
            if t < 2:
                product(a[:], w1d[t], slice(0, P), xq, slice(0, R))
            else:
                product(a[:], w1d_late, cols(t - 2), xq, slice(0, R))
            scale = (ts_early if t < PACK - 1 else ts_cols)[:, t : t + 1]
            nc.vector.scalar_tensor_tensor(out=z[:, t, :], in0=a[:], scalar=scale, in1=us_row[:], op0=ALU.mult, op1=ALU.mult)
            nc.scalar.activation(out=th[:, t, :], in_=z[:, t, :], func=ACT.Tanh, scale=0.5)
            nc.scalar.activation(out=m[:, t, :], in_=z[:, t, :], func=ACT.Silu, scale=-1.0)
        turn1 = turn(1, 0)

        gate = sb("gate", [P, PACK, R], F32)
        f = sb("f", [P, PACK, R], F32)

        def form_gate(part):
            nc.vector.scalar_tensor_tensor(out=gate[:, part, :], in0=th[:, part, :], scalar=1.0, in1=table[:, part, :], op0=ALU.add, op1=ALU.mult)

        def form_f(part):
            nc.vector.scalar_tensor_tensor(out=f[:, part, :], in0=m[:, part, :], scalar=1.0, in1=gate[:, part, :], op0=ALU.subtract, op1=ALU.mult)

        w2_listed = at(4096, "w2_listed", [P, PACK, S], BF16)
        nc.vector.tensor_copy(out=w2_listed[:, 0, :], in_=w2_planes[0][:].indirect(offsets[:]))
        nc.vector.tensor_copy(out=w2_listed[:, 1, 0:128], in_=w2_planes[1][:].indirect(offsets[:, 0:8]))
        nc.scalar.activation(out=w2_listed[:, 1, 128:S], in_=w2_planes[1][:].indirect(offsets[:, 8:32]), func=ACT.Copy)
        for j in range(2, PACK):
            nc.scalar.activation(out=w2_listed[:, j, :], in_=w2_planes[j][:].indirect(offsets[:]), func=ACT.Copy)
        form_gate(slice(0, 2))
        dyq = [quantize("dyq0", dy_first[:].rearrange("p r j -> p (r j)"), R // 2, E5M2)]
        form_f(slice(0, 2))
        for form in (form_gate, form_f):
            for t in (2, 3):
                form(slice(t, t + 1))

        w2_woven = sb("w2_woven", [P, S, PACK], BF16)

        def weave_w2(copy, w, part):
            copy(
                out=w2_woven[:].rearrange("p (t g i) j -> p g t i j", t=PACK, i=2)[:, part, 2 * w : 2 * w + 2],
                in_=w2_listed[:].rearrange("p j (g i t) -> p g t i j", t=PACK, i=2)[:, part, 2 * w : 2 * w + 2],
            )

        weave_w2(nc.vector.tensor_copy, 0, slice(0, 64))
        weave_w2(nc.vector.tensor_copy, 1, slice(0, 32))
        weave_w2(nc.scalar.copy, 1, slice(32, 64))
        dy_second = sb("dy_second", [P, R // 2, PACK], BF16, "w2_plane3")
        nc.scalar.copy(
            out=dy_second[:].rearrange("p (g i) j -> p g j i", i=4), in_=dy_halves[1][:].rearrange("p j (g i) -> p g j i", i=4)
        )
        woven_flat = w2_woven[:].rearrange("p s j -> p (s j)")
        w2e = [quantize(f"w2e{w}", woven_flat[:, cols(w, 1024)], 256, E4M3) for w in range(2)]
        dyq.append(quantize("dyq1", dy_second[:].rearrange("p r j -> p (r j)"), R // 2, E5M2, 4096))
        turned1 = copy_turned(1, turn1, "w2_plane3")

        half = R // 2
        dhs = [[bank(4 + 2 * h + w, f"dh{h}{w}", [P, 2, half]) for w in range(2)] for h in range(2)]
        for h in range(2):
            for w in range(2):
                for e in range(2):
                    product(dhs[h][w][:, e, :], w2e[w], cols(e), dyq[h], slice(0, half))

        def form_da(target, w, first, count):
            h, start = divmod(first, half)
            nc.vector.tensor_tensor(
                out=target.rearrange("q (g i) e -> q g e i", i=4),
                in0=dhs[h][w][:, :, start : start + count].rearrange("q e (g i) -> q g e i", i=4),
                in1=f[:, 2 * w : 2 * w + 2, first : first + count].rearrange("q e (g i) -> q g e i", i=4),
                op=ALU.mult,
            )

        def form_in_pairs(name, first, count):
            pairs = sb(name + "_pairs", [P, 2, count * 2], BF16)
            for w in range(2):
                form_da(pairs[:, w, :].rearrange("q (r e) -> q r e", e=2), w, first, count)
            woven = sb(name + "_woven", [P, count * PACK], BF16)
            nc.scalar.copy(
                out=woven[:].bitcast(F32).rearrange("q (r w) -> q r w", w=2), in_=pairs[:].bitcast(F32).rearrange("q w r -> q r w")
            )
            return woven

        def finish(c, woven):
            daq = quantize(f"daq{c}", woven, P, E5M2)
            acc = bank(c, f"acc{c}", [P, D])
            for b in range(2):
                product(acc[:, cols(b, 256)], daq, slice(0, P), w1i[b], slice(0, 256))
            res = sb(f"res{c}", [P, D], F32)
            res_view = res[:].rearrange("r (p b j) -> r p b j", b=2, j=2)
            acc_view = acc[:].rearrange("r (b p j) -> r p b j", b=2, j=2)
            if c < CHUNKS - 1:
                nc.scalar.copy(out=res_view, in_=acc_view)
                nc.sync.dma_start(out[cols(c), :], res[:])
            else:
                for k in range(2):
                    nc.vector.tensor_copy(out=res_view[:, cols(k, 64)], in_=acc_view[:, cols(k, 64)])
                    nc.sync.dma_start(out[cols(c), cols(k, 256)], res[:, cols(k, 256)])

        das = [form_in_pairs(f"da{c}", c * P, P) for c in range(2)]
        w1i.append(quantize("w1i1", turned1[:], D // 2, E4M3))
        finish(0, das[0][:])
        das.append(form_in_pairs("da2", 2 * P, P))
        finish(1, das[1][:])
        da_last = sb("da_last", [P, P, PACK], BF16)
        for w in range(2):
            form_da(da_last[:, :, 2 * w : 2 * w + 2], w, R - P, P)
        finish(2, das[2][:])
        finish(3, da_last[:].rearrange("q r t -> q (r t)"))
